import numpy as np
import ml_dtypes


def mxq(x, axis, fmt="e4m3"):
    dtype, down = {"e4m3": (ml_dtypes.float8_e4m3fn, 7), "e5m2": (ml_dtypes.float8_e5m2, 14)}[fmt]
    v = np.moveaxis(np.asarray(x, np.float32).astype(ml_dtypes.bfloat16).astype(np.float64), axis, -1)
    blocks = v.reshape(v.shape[:-1] + (-1, 32))
    amax = np.abs(blocks).max(-1, keepdims=True)
    byte = np.maximum(np.where(amax > 0, np.frexp(amax)[1] - 1 + 127, 0) - down, 1)
    scale = np.exp2(byte - 127.0)
    codes = (blocks / scale).astype(np.float32).astype(dtype).astype(np.float64)
    return np.moveaxis((codes * scale).reshape(v.shape), -1, axis)


WIDE = False


def mx_kscale(k):
    if not WIDE:
        return np.ones(k)
    levels = np.array([10, -10, 5, -5, 0])
    if k % 512:
        return np.exp2(np.random.permutation(np.resize(levels, k // 32))).repeat(32)
    a = np.empty((k // 512, 16))
    for p in range(k // 512):
        a[p, :8] = np.random.permutation(np.resize(levels, 8))
        for g in range(8):
            far = levels[np.abs(levels - a[p, g]) >= 10]
            a[p, g + 8] = far[np.random.randint(len(far))]
    return np.exp2(a.ravel()).repeat(32)


def f64(x):
    return np.asarray(x).astype(np.float64)


def striped8(idx):
    return np.concatenate([v.reshape(-1, 16).T for v in idx]).astype(np.uint16)


def unstriped8(offs):
    return np.stack([offs[16 * g:16 * g + 16].T.reshape(-1) for g in range(8)]).astype(np.int64)


E2M1 = np.array([0.0, 0.5, 1.0, 1.5, 2.0, 3.0, 4.0, 6.0, -0.0, -0.5, -1.0, -1.5, -2.0, -3.0, -4.0, -6.0])


def pack_weight(w, fmt):
    k, n = w.shape
    w = f64(np.asarray(w, np.float32).astype(ml_dtypes.bfloat16)).reshape(k // 32, 32, n)
    amax = np.abs(w).max(1)
    if fmt == "e4m3":
        byte = np.frexp(amax)[1] - 1 + 127 - 7
    else:
        mant, ex = np.frexp(amax / 6.0)
        byte = np.where(mant > 0.5, ex, ex - 1) + 127
    byte = np.clip(np.where(amax > 0, byte, 1), 1, 254)
    scaled = (w * np.exp2(127.0 - byte)[:, None, :]).reshape(k, n).astype(np.float32)
    by_word = np.ascontiguousarray(scaled.reshape(k // 512, 128, 4, n).transpose(0, 1, 3, 2))
    if fmt == "e4m3":
        words = by_word.astype(ml_dtypes.float8_e4m3fn).view(np.uint8)
    else:
        c = by_word.astype(ml_dtypes.float4_e2m1fn).view(np.uint8) & 0xF
        words = (c[..., 0::2] | (c[..., 1::2] << 4)).reshape(k // 512, 128, 2 * n)
    return np.ascontiguousarray(words), np.ascontiguousarray(byte.astype(np.uint8).reshape(k // 512, 16, n))


def unpack_weight(words, scales, fmt):
    g, _, n = scales.shape
    words = np.ascontiguousarray(words).reshape(g, 128, n, -1)
    if fmt == "e4m3":
        vals = words.view(ml_dtypes.float8_e4m3fn).astype(np.float64)
    else:
        nib = np.empty((g, 128, n, 4), np.uint8)
        nib[..., 0::2] = words & 0xF
        nib[..., 1::2] = words >> 4
        vals = E2M1[nib]
    vals = vals * np.repeat(np.exp2(scales.astype(np.float64) - 127.0), 8, axis=1)[..., None]
    return vals.transpose(0, 1, 3, 2).reshape(g * 512, n)


K, M, T, S = 2048, 256, 512, 256


def setup_inputs():
    n = np.random.standard_normal
    s = mx_kscale(K)[:, None]
    p_w = pack_weight(n((K, M)) / np.sqrt(K) / s, "e4m3")
    return {
        "x": (n((K, S)) * s).astype(np.float32),
        "w_words": p_w[0],
        "w_scales": p_w[1],
        "wgo": np.repeat(np.random.uniform(0.5, 2.0, (8, S)), 16, axis=0).astype(np.float32),
        "offs": striped8(np.stack([np.random.permutation(T)[:S] for _ in range(8)])),
    }


def reference(x, w_words, w_scales, wgo, offs):
    x_ = mxq(f64(x), 0, "e4m3")
    w_ = unpack_weight(w_words, w_scales, "e4m3")
    y = w_.T @ x_
    place = unstriped8(offs)[np.arange(M) % 128 // 16]
    out = np.zeros((M, T))
    out[np.arange(M)[:, None], place] = f64(wgo)[np.arange(M) % 128] * (y)
    return out

@@ -1,0 +1,165 @@
+from contextlib import ExitStack
+
+import concourse.mybir as mybir
+
+K, M, S, T = 2048, 256, 256, 512
+FLOPS = 2 * K * M * S
+
+F32 = mybir.dt.float32
+BF16 = mybir.dt.bfloat16
+U32 = mybir.dt.uint32
+I32 = mybir.dt.int32
+U16 = mybir.dt.uint16
+U8 = mybir.dt.uint8
+FP8X4 = mybir.dt.float8_e4m3fn_x4
+MULT = mybir.AluOpType.mult
+
+P = 128
+PACK = 4
+K_PASS = P * PACK
+PASSES = K // K_PASS
+HALF = S // 2
+HALVES = S // HALF
+M_TILES = M // P
+
+
+def tile_list_hscat_none_kernel(tc, x, w_words, w_scales, wgo, offs, out):
+    nc = tc.nc
+    with ExitStack() as ctx:
+        keep = ctx.enter_context(tc.tile_pool(name="keep", bufs=1))
+        psum = ctx.enter_context(tc.psum_pool(name="psum", bufs=1))
+
+        def load_x(a, c0, width):
+            raw = keep.tile([P, PACK, width], F32, name=f"raw_{a}_{c0}", align_bytes=64)
+            rows = x[a * K_PASS : (a + 1) * K_PASS, c0 : c0 + width]
+            nc.sync.dma_start(out=raw[:], in_=rows.rearrange("(p j) w -> p j w", j=PACK))
+            grouped = keep.tile([P, width, PACK], BF16, name=f"grouped_{a}_{c0}", align_bytes=64)
+            return raw, grouped
+
+        def interleave(copy, chunk, c0, c1):
+            raw, grouped = chunk
+            copy(
+                out=grouped[:, c0:c1, :].rearrange("p (c i) t -> p c t i", i=4),
+                in_=raw[:, :, c0:c1].rearrange("p t (c i) -> p c t i", i=4),
+            )
+
+        def quantize(a, c0, width, chunk):
+            codes = keep.tile([P, width], U32, name=f"codes_{a}_{c0}", align_bytes=64)
+            scales = keep.tile([P, width], U8, name=f"scales_{a}_{c0}", align_bytes=64)
+            nc.vector.quantize_mx(
+                out=codes[:].bitcast(FP8X4),
+                scales=scales[:],
+                in_=chunk[1][:].rearrange("p w t -> p (w t)"),
+            )
+            return codes, scales
+
+        packed = keep.tile([P, M], U8, name="packed", align_bytes=64)
+        nc.gpsimd.memset(packed[:].bitcast(I32), 0)
+        windows = [keep.tile([P, T], F32, name=f"window_{m}", align_bytes=64) for m in range(M_TILES)]
+        for m in range(M_TILES):
+            nc.gpsimd.memset(windows[m][:], 0.0)
+
+        offsets = keep.tile([P, S // 16], U16, name="offsets")
+        weights = keep.tile([P, S], F32, name="weights", align_bytes=64)
+        words = [keep.tile([P, PASSES, P], U32, name=f"words_{m}", align_bytes=64) for m in range(M_TILES)]
+
+        def load_w(m):
+            nc.sync.dma_start(
+                out=words[m][:].bitcast(I32),
+                in_=w_words[:, :, m * P : (m + 1) * P, :].rearrange("a p n t -> p a (n t)").bitcast(I32),
+            )
+
+        def load_scales(q):
+            nc.sync.dma_start(
+                out=packed[32 * q : 32 * q + 16, :].bitcast(I32),
+                in_=w_scales[:, 4 * q : 4 * q + 4, :].bitcast(I32),
+            )
+
+        x_in = {}
+        nc.sync.dma_start(offsets[:], offs)
+        x_in[0, 0] = load_x(0, 0, S)
+        load_scales(0)
+        load_scales(1)
+        load_scales(2)
+        load_scales(3)
+        x_in[1, 0] = load_x(1, 0, S)
+        x_in[2, 0] = load_x(2, 0, S)
+        load_w(0)
+        x_in[3, 0] = load_x(3, 0 * HALF, HALF)
+        nc.sync.dma_start(out=weights[:], in_=wgo)
+        x_in[3, 1] = load_x(3, 1 * HALF, HALF)
+        load_w(1)
+
+        acc = [[psum.tile([P, HALF], F32, name=f"acc_{m}_{h}") for h in range(HALVES)] for m in range(M_TILES)]
+        results = [[keep.tile([P, HALF], F32, name=f"y_{m}_{h}", align_bytes=64) for h in range(HALVES)] for m in range(M_TILES)]
+        quantized = {}
+
+        def multiply(a, m, h):
+            codes, scales, c0 = quantized[a, h]
+            nc.tensor.matmul_mx(
+                out=acc[m][h][:],
+                lhsT=words[m][:, a, :].bitcast(FP8X4),
+                lhsT_scale=packed[4 * a :, m * P : (m + 1) * P],
+                rhs=codes[:, c0 : c0 + HALF].bitcast(FP8X4),
+                rhs_scale=scales[:, c0 : c0 + HALF],
+                start=(a == 0),
+                stop=(a == PASSES - 1),
+            )
+
+        def place(m, h):
+            nc.vector.tensor_tensor(
+                windows[m][:].indirect(offsets[:, 8 * h : 8 * h + 8]),
+                results[m][h][:],
+                weights[:, h * HALF : (h + 1) * HALF],
+                MULT,
+            )
+
+        def store(m):
+            nc.sync.dma_start(out=out[m * P : (m + 1) * P, :], in_=windows[m][:])
+
+        def cast(a, h, width, vector_cols):
+            if vector_cols > 0:
+                interleave(nc.vector.tensor_copy, x_in[a, h], 0, vector_cols)
+            if vector_cols < width:
+                interleave(nc.scalar.copy, x_in[a, h], vector_cols, width)
+
+        def fetch(m, h):
+            nc.scalar.copy(out=results[m][h][:], in_=acc[m][h][:])
+
+        def quant(a, h, width):
+            codes, scales = quantize(a, h * HALF, width, x_in[a, h])
+            for i in range(width // HALF):
+                quantized[a, h + i] = (codes, scales, i * HALF)
+
+        cast(0, 0, S, 176)
+        quant(0, 0, S)
+        multiply(0, 0, 0)
+        multiply(0, 0, 1)
+        cast(1, 0, S, 176)
+        quant(1, 0, S)
+        multiply(1, 0, 0)
+        multiply(1, 0, 1)
+        cast(2, 0, S, 176)
+        quant(2, 0, S)
+        multiply(2, 0, 0)
+        multiply(2, 0, 1)
+        cast(3, 0, HALF, 44)
+        quant(3, 0, HALF)
+        multiply(3, 0, 0)
+        fetch(0, 0)
+        place(0, 0)
+        cast(3, 1, HALF, 0)
+        quant(3, 1, HALF)
+        for a in range(PASSES):
+            multiply(a, 1, 0)
+        fetch(1, 0)
+        multiply(3, 0, 1)
+        place(1, 0)
+        fetch(0, 1)
+        place(0, 1)
+        store(0)
+        for a in range(PASSES):
+            multiply(a, 1, 1)
+        fetch(1, 1)
+        place(1, 1)
+        store(1)

@@ -76,19 +76,18 @@ def tile_list_hscat_none_kernel(tc, x, w_words, w_scales, wgo, offs, out):
             )
 
         x_in = {}
-        nc.sync.dma_start(offsets[:], offs)
-        x_in[0, 0] = load_x(0, 0, S)
-        load_scales(0)
-        load_scales(1)
-        load_scales(2)
-        load_scales(3)
-        x_in[1, 0] = load_x(1, 0, S)
-        x_in[2, 0] = load_x(2, 0, S)
+        x_in[0, 0] = load_x(0, 0, HALF)
+        for q in range(4):
+            load_scales(q)
+        x_in[1, 0] = load_x(1, 0, HALF)
         load_w(0)
-        x_in[3, 0] = load_x(3, 0 * HALF, HALF)
+        x_in[2, 0] = load_x(2, 0, HALF)
+        x_in[3, 0] = load_x(3, 0, HALF)
+        nc.sync.dma_start(offsets[:], offs)
         nc.sync.dma_start(out=weights[:], in_=wgo)
-        x_in[3, 1] = load_x(3, 1 * HALF, HALF)
         load_w(1)
+        for a in range(PASSES):
+            x_in[a, 1] = load_x(a, HALF, HALF)
 
         acc = [[psum.tile([P, HALF], F32, name=f"acc_{m}_{h}") for h in range(HALVES)] for m in range(M_TILES)]
         results = [[keep.tile([P, HALF], F32, name=f"y_{m}_{h}", align_bytes=64) for h in range(HALVES)] for m in range(M_TILES)]
@@ -131,35 +130,22 @@ def tile_list_hscat_none_kernel(tc, x, w_words, w_scales, wgo, offs, out):
             for i in range(width // HALF):
                 quantized[a, h + i] = (codes, scales, i * HALF)
 
-        cast(0, 0, S, 176)
-        quant(0, 0, S)
-        multiply(0, 0, 0)
-        multiply(0, 0, 1)
-        cast(1, 0, S, 176)
-        quant(1, 0, S)
-        multiply(1, 0, 0)
-        multiply(1, 0, 1)
-        cast(2, 0, S, 176)
-        quant(2, 0, S)
-        multiply(2, 0, 0)
-        multiply(2, 0, 1)
-        cast(3, 0, HALF, 44)
-        quant(3, 0, HALF)
-        multiply(3, 0, 0)
+        for a in range(PASSES):
+            cast(a, 0, HALF, 88)
+            quant(a, 0, HALF)
+            multiply(a, 0, 0)
         fetch(0, 0)
         place(0, 0)
-        cast(3, 1, HALF, 0)
-        quant(3, 1, HALF)
         for a in range(PASSES):
             multiply(a, 1, 0)
         fetch(1, 0)
-        multiply(3, 0, 1)
         place(1, 0)
-        fetch(0, 1)
-        place(0, 1)
-        store(0)
         for a in range(PASSES):
+            cast(a, 1, HALF, 88 if a == PASSES - 1 else 0)
+            quant(a, 1, HALF)
+            multiply(a, 0, 1)
             multiply(a, 1, 1)
-        fetch(1, 1)
-        place(1, 1)
-        store(1)
+        for m in range(M_TILES):
+            fetch(m, 1)
+            place(m, 1)
+            store(m)

@@ -21,6 +21,7 @@ PASSES = K // K_PASS
 HALF = S // 2
 HALVES = S // HALF
 M_TILES = M // P
+LAST = PASSES - 1
 
 
 def tile_list_hscat_none_kernel(tc, x, w_words, w_scales, wgo, offs, out):
@@ -29,39 +30,23 @@ def tile_list_hscat_none_kernel(tc, x, w_words, w_scales, wgo, offs, out):
         keep = ctx.enter_context(tc.tile_pool(name="keep", bufs=1))
         psum = ctx.enter_context(tc.psum_pool(name="psum", bufs=1))
 
-        def load_x(a, c0, width):
-            raw = keep.tile([P, PACK, width], F32, name=f"raw_{a}_{c0}", align_bytes=64)
-            rows = x[a * K_PASS : (a + 1) * K_PASS, c0 : c0 + width]
-            nc.sync.dma_start(out=raw[:], in_=rows.rearrange("(p j) w -> p j w", j=PACK))
-            grouped = keep.tile([P, width, PACK], BF16, name=f"grouped_{a}_{c0}", align_bytes=64)
-            return raw, grouped
+        def tile(shape, dtype, name, tag=None):
+            return keep.tile(shape, dtype, name=name, tag=tag or name, align_bytes=64)
 
-        def interleave(copy, chunk, c0, c1):
-            raw, grouped = chunk
-            copy(
-                out=grouped[:, c0:c1, :].rearrange("p (c i) t -> p c t i", i=4),
-                in_=raw[:, :, c0:c1].rearrange("p t (c i) -> p c t i", i=4),
-            )
-
-        def quantize(a, c0, width, chunk):
-            codes = keep.tile([P, width], U32, name=f"codes_{a}_{c0}", align_bytes=64)
-            scales = keep.tile([P, width], U8, name=f"scales_{a}_{c0}", align_bytes=64)
-            nc.vector.quantize_mx(
-                out=codes[:].bitcast(FP8X4),
-                scales=scales[:],
-                in_=chunk[1][:].rearrange("p w t -> p (w t)"),
-            )
-            return codes, scales
-
-        packed = keep.tile([P, M], U8, name="packed", align_bytes=64)
-        nc.gpsimd.memset(packed[:].bitcast(I32), 0)
-        windows = [keep.tile([P, T], F32, name=f"window_{m}", align_bytes=64) for m in range(M_TILES)]
+        packed = tile([P, M], U8, "packed")
+        windows = [tile([P, T], F32, f"window_{m}") for m in range(M_TILES)]
         for m in range(M_TILES):
             nc.gpsimd.memset(windows[m][:], 0.0)
 
         offsets = keep.tile([P, S // 16], U16, name="offsets")
-        weights = keep.tile([P, S], F32, name="weights", align_bytes=64)
-        words = [keep.tile([P, PASSES, P], U32, name=f"words_{m}", align_bytes=64) for m in range(M_TILES)]
+        weights = [tile([P, HALF], F32, f"weights_{h}") for h in range(HALVES)]
+        words = [tile([P, PASSES, P], U32, f"words_{m}") for m in range(M_TILES)]
+        raw = {}
+
+        def load_x(a, h, tag=None):
+            raw[a, h] = tile([P, PACK, HALF], F32, f"raw_{a}_{h}", tag)
+            rows = x[a * K_PASS : (a + 1) * K_PASS, h * HALF : (h + 1) * HALF]
+            nc.sync.dma_start(out=raw[a, h][:], in_=rows.rearrange("(p j) w -> p j w", j=PACK))
 
         def load_w(m):
             nc.sync.dma_start(
@@ -70,81 +55,109 @@ def tile_list_hscat_none_kernel(tc, x, w_words, w_scales, wgo, offs, out):
             )
 
         def load_scales(q):
-            nc.sync.dma_start(
+            nc.scalar.dma_start(
                 out=packed[32 * q : 32 * q + 16, :].bitcast(I32),
                 in_=w_scales[:, 4 * q : 4 * q + 4, :].bitcast(I32),
             )
 
-        x_in = {}
-        x_in[0, 0] = load_x(0, 0, HALF)
+        def load_weights(h):
+            nc.sync.dma_start(out=weights[h][:], in_=wgo[:, h * HALF : (h + 1) * HALF])
+
         for q in range(4):
             load_scales(q)
-        x_in[1, 0] = load_x(1, 0, HALF)
-        load_w(0)
-        x_in[2, 0] = load_x(2, 0, HALF)
-        x_in[3, 0] = load_x(3, 0, HALF)
-        nc.sync.dma_start(offsets[:], offs)
-        nc.sync.dma_start(out=weights[:], in_=wgo)
-        load_w(1)
         for a in range(PASSES):
-            x_in[a, 1] = load_x(a, HALF, HALF)
+            load_x(a, 0)
+        load_w(0)
+        load_x(0, 1)
+        load_weights(0)
+        load_x(1, 1)
+        nc.sync.dma_start(offsets[:], offs)
+        load_w(1)
+        load_x(2, 1)
+        load_x(3, 1, "last_rows")
+        load_weights(1)
 
         acc = [[psum.tile([P, HALF], F32, name=f"acc_{m}_{h}") for h in range(HALVES)] for m in range(M_TILES)]
-        results = [[keep.tile([P, HALF], F32, name=f"y_{m}_{h}", align_bytes=64) for h in range(HALVES)] for m in range(M_TILES)]
+        results = {}
+        interleaved = {}
         quantized = {}
 
+        def interleave(copy, a, h, grouped, c0, c1):
+            copy(
+                out=grouped[:, c0:c1, :].rearrange("p (c i) t -> p c t i", i=4),
+                in_=raw[a, h][:, :, c0:c1].rearrange("p t (c i) -> p c t i", i=4),
+            )
+
+        def cast(a, h, vector_cols, tag=None):
+            grouped = tile([P, HALF, PACK], BF16, f"grouped_{a}_{h}", tag)[:]
+            interleaved[a, h] = grouped
+            if vector_cols > 0:
+                interleave(nc.vector.tensor_copy, a, h, grouped, 0, vector_cols)
+            if vector_cols < HALF:
+                interleave(nc.scalar.copy, a, h, grouped, vector_cols, HALF)
+
+        def quantize(a, h, tag=None):
+            codes = tile([P, HALF], U32, f"codes_{a}_{h}", tag)
+            scales = tile([P, HALF], U8, f"scales_{a}_{h}")
+            nc.vector.quantize_mx(
+                out=codes[:].bitcast(FP8X4),
+                scales=scales[:],
+                in_=interleaved[a, h].rearrange("p w t -> p (w t)"),
+            )
+            quantized[a, h] = (codes, scales)
+
         def multiply(a, m, h):
-            codes, scales, c0 = quantized[a, h]
+            codes, scales = quantized[a, h]
             nc.tensor.matmul_mx(
                 out=acc[m][h][:],
                 lhsT=words[m][:, a, :].bitcast(FP8X4),
                 lhsT_scale=packed[4 * a :, m * P : (m + 1) * P],
-                rhs=codes[:, c0 : c0 + HALF].bitcast(FP8X4),
-                rhs_scale=scales[:, c0 : c0 + HALF],
+                rhs=codes[:].bitcast(FP8X4),
+                rhs_scale=scales[:],
                 start=(a == 0),
-                stop=(a == PASSES - 1),
+                stop=(a == LAST),
             )
+
+        def fetch(m, h, tag=None):
+            results[m, h] = tile([P, HALF], F32, f"y_{m}_{h}", tag)
+            nc.scalar.copy(out=results[m, h][:], in_=acc[m][h][:])
 
         def place(m, h):
             nc.vector.tensor_tensor(
                 windows[m][:].indirect(offsets[:, 8 * h : 8 * h + 8]),
-                results[m][h][:],
-                weights[:, h * HALF : (h + 1) * HALF],
+                results[m, h][:],
+                weights[h][:],
                 MULT,
             )
 
         def store(m):
             nc.sync.dma_start(out=out[m * P : (m + 1) * P, :], in_=windows[m][:])
 
-        def cast(a, h, width, vector_cols):
-            if vector_cols > 0:
-                interleave(nc.vector.tensor_copy, x_in[a, h], 0, vector_cols)
-            if vector_cols < width:
-                interleave(nc.scalar.copy, x_in[a, h], vector_cols, width)
-
-        def fetch(m, h):
-            nc.scalar.copy(out=results[m][h][:], in_=acc[m][h][:])
-
-        def quant(a, h, width):
-            codes, scales = quantize(a, h * HALF, width, x_in[a, h])
-            for i in range(width // HALF):
-                quantized[a, h + i] = (codes, scales, i * HALF)
-
         for a in range(PASSES):
-            cast(a, 0, HALF, 88)
-            quant(a, 0, HALF)
+            cast(a, 0, HALF)
+            quantize(a, 0)
             multiply(a, 0, 0)
-        fetch(0, 0)
+        fetch(0, 0, "first_result")
+        for a in range(2):
+            cast(a, 1, HALF)
+            quantize(a, 1)
         place(0, 0)
+        cast(2, 1, 0)
+        cast(3, 1, HALF, "first_result")
+        quantize(2, 1)
+        quantize(3, 1)
+        for a in range(2):
+            multiply(a, 0, 1)
         for a in range(PASSES):
             multiply(a, 1, 0)
-        fetch(1, 0)
-        place(1, 0)
-        for a in range(PASSES):
-            cast(a, 1, HALF, 88 if a == PASSES - 1 else 0)
-            quant(a, 1, HALF)
-            multiply(a, 0, 1)
+        for a in range(2):
             multiply(a, 1, 1)
+        multiply(2, 0, 1)
+        multiply(2, 1, 1)
+        multiply(LAST, 0, 1)
+        multiply(LAST, 1, 1)
+        fetch(1, 0, "last_rows")
+        place(1, 0)
         for m in range(M_TILES):
             fetch(m, 1)
             place(m, 1)

@@ -39,126 +39,138 @@ def tile_list_hscat_none_kernel(tc, x, w_words, w_scales, wgo, offs, out):
             nc.gpsimd.memset(windows[m][:], 0.0)
 
         offsets = keep.tile([P, S // 16], U16, name="offsets")
-        weights = [tile([P, HALF], F32, f"weights_{h}") for h in range(HALVES)]
-        words = [tile([P, PASSES, P], U32, f"words_{m}") for m in range(M_TILES)]
+        all_weights = tile([P, S], F32, "all_weights")
+        weights = {}
+        words = {}
         raw = {}
 
-        def load_x(a, h, tag=None):
-            raw[a, h] = tile([P, PACK, HALF], F32, f"raw_{a}_{h}", tag)
-            rows = x[a * K_PASS : (a + 1) * K_PASS, h * HALF : (h + 1) * HALF]
-            nc.sync.dma_start(out=raw[a, h][:], in_=rows.rearrange("(p j) w -> p j w", j=PACK))
+        def load_x(a, h, width, tag=None):
+            loaded = tile([P, PACK, width], F32, f"raw_{a}_{h}", tag)
+            rows = x[a * K_PASS : (a + 1) * K_PASS, h * HALF : h * HALF + width]
+            nc.sync.dma_start(out=loaded[:], in_=rows.rearrange("(p j) w -> p j w", j=PACK))
+            for i in range(width // HALF):
+                raw[a, h + i] = loaded[:, :, i * HALF :]
 
-        def load_w(m):
+        def load_w(m0, m1, a0, a1):
+            both = tile([P, a1 - a0, (m1 - m0) * P], U32, f"words_{m0}_{a0}")
             nc.sync.dma_start(
-                out=words[m][:].bitcast(I32),
-                in_=w_words[:, :, m * P : (m + 1) * P, :].rearrange("a p n t -> p a (n t)").bitcast(I32),
+                out=both[:].bitcast(I32),
+                in_=w_words[a0:a1, :, m0 * P : m1 * P, :].rearrange("a p n t -> p a (n t)").bitcast(I32),
             )
+            for m in range(m0, m1):
+                for a in range(a0, a1):
+                    words[m, a] = both[:, a - a0, (m - m0) * P : (m - m0 + 1) * P]
 
         def load_scales(q):
-            nc.scalar.dma_start(
+            nc.sync.dma_start(
                 out=packed[32 * q : 32 * q + 16, :].bitcast(I32),
                 in_=w_scales[:, 4 * q : 4 * q + 4, :].bitcast(I32),
             )
 
-        def load_weights(h):
-            nc.sync.dma_start(out=weights[h][:], in_=wgo[:, h * HALF : (h + 1) * HALF])
+        def load_weights(h0, h1):
+            nc.sync.dma_start(out=all_weights[:, h0 * HALF : h1 * HALF], in_=wgo[:, h0 * HALF : h1 * HALF])
+            for h in range(h0, h1):
+                weights[h] = all_weights[:, h * HALF : (h + 1) * HALF]
 
-        for q in range(4):
+        load_x(0, 0, S)
+        for q in range(3):
             load_scales(q)
-        for a in range(PASSES):
-            load_x(a, 0)
-        load_w(0)
-        load_x(0, 1)
-        load_weights(0)
-        load_x(1, 1)
+        load_x(1, 0, S)
+        load_x(2, 0, S)
+        load_x(LAST, 0, HALF)
+        load_w(0, 1, 0, PASSES)
+        load_scales(3)
+        load_w(1, 2, 0, PASSES)
+        load_x(LAST, 1, HALF)
         nc.sync.dma_start(offsets[:], offs)
-        load_w(1)
-        load_x(2, 1)
-        load_x(3, 1, "last_rows")
-        load_weights(1)
+        load_weights(0, HALVES)
 
-        acc = [[psum.tile([P, HALF], F32, name=f"acc_{m}_{h}") for h in range(HALVES)] for m in range(M_TILES)]
+        acc = {}
         results = {}
         interleaved = {}
         quantized = {}
 
-        def interleave(copy, a, h, grouped, c0, c1):
+        def interleave(copy, a, h, c0, c1):
             copy(
-                out=grouped[:, c0:c1, :].rearrange("p (c i) t -> p c t i", i=4),
+                out=interleaved[a, h][:, c0:c1, :].rearrange("p (c i) t -> p c t i", i=4),
                 in_=raw[a, h][:, :, c0:c1].rearrange("p t (c i) -> p c t i", i=4),
             )
 
-        def cast(a, h, vector_cols, tag=None):
-            grouped = tile([P, HALF, PACK], BF16, f"grouped_{a}_{h}", tag)[:]
-            interleaved[a, h] = grouped
+        def cast(a, h, width, vector_cols, tag=None):
+            interleaved[a, h] = tile([P, width, PACK], BF16, f"grouped_{a}_{h}", tag)
             if vector_cols > 0:
-                interleave(nc.vector.tensor_copy, a, h, grouped, 0, vector_cols)
-            if vector_cols < HALF:
-                interleave(nc.scalar.copy, a, h, grouped, vector_cols, HALF)
+                interleave(nc.vector.tensor_copy, a, h, 0, vector_cols)
+            if vector_cols < width:
+                interleave(nc.scalar.copy, a, h, vector_cols, width)
 
-        def quantize(a, h, tag=None):
-            codes = tile([P, HALF], U32, f"codes_{a}_{h}", tag)
-            scales = tile([P, HALF], U8, f"scales_{a}_{h}")
+        def quantize(a, h, width, tag=None):
+            codes = tile([P, width], U32, f"codes_{a}_{h}", tag)
+            scales = tile([P, width], U8, f"scales_{a}_{h}")
+            whole = (a, h) if (a, h) in interleaved else (a, 0)
+            c0 = (h - whole[1]) * HALF
             nc.vector.quantize_mx(
                 out=codes[:].bitcast(FP8X4),
                 scales=scales[:],
-                in_=interleaved[a, h].rearrange("p w t -> p (w t)"),
+                in_=interleaved[whole][:, c0 : c0 + width, :].rearrange("p w t -> p (w t)"),
             )
-            quantized[a, h] = (codes, scales)
+            for i in range(width // HALF):
+                cols = slice(i * HALF, (i + 1) * HALF)
+                quantized[a, h + i] = (codes[:, cols], scales[:, cols])
 
-        def multiply(a, m, h):
+        def multiply(a, m, h, start, stop):
             codes, scales = quantized[a, h]
             nc.tensor.matmul_mx(
-                out=acc[m][h][:],
-                lhsT=words[m][:, a, :].bitcast(FP8X4),
+                out=acc[m, h][:],
+                lhsT=words[m, a].bitcast(FP8X4),
                 lhsT_scale=packed[4 * a :, m * P : (m + 1) * P],
-                rhs=codes[:].bitcast(FP8X4),
-                rhs_scale=scales[:],
-                start=(a == 0),
-                stop=(a == LAST),
+                rhs=codes.bitcast(FP8X4),
+                rhs_scale=scales,
+                start=start,
+                stop=stop,
             )
+
+        def product(m, h, order, bank):
+            acc[m, h] = psum.tile([P, HALF], F32, name=f"acc_{m}_{h}", tag=bank)
+            for a in order:
+                multiply(a, m, h, a == order[0], a == order[-1])
 
         def fetch(m, h, tag=None):
             results[m, h] = tile([P, HALF], F32, f"y_{m}_{h}", tag)
-            nc.scalar.copy(out=results[m, h][:], in_=acc[m][h][:])
+            nc.scalar.copy(out=results[m, h][:], in_=acc[m, h][:])
 
         def place(m, h):
             nc.vector.tensor_tensor(
                 windows[m][:].indirect(offsets[:, 8 * h : 8 * h + 8]),
                 results[m, h][:],
-                weights[h][:],
+                weights[h],
                 MULT,
             )
 
         def store(m):
             nc.sync.dma_start(out=out[m * P : (m + 1) * P, :], in_=windows[m][:])
 
-        for a in range(PASSES):
-            cast(a, 0, HALF)
-            quantize(a, 0)
-            multiply(a, 0, 0)
-        fetch(0, 0, "first_result")
         for a in range(2):
-            cast(a, 1, HALF)
-            quantize(a, 1)
+            cast(a, 0, S, 176)
+            quantize(a, 0, S)
+        cast(2, 0, HALF, 88)
+        quantize(2, 0, HALF)
+        cast(2, 1, HALF, 0)
+        cast(LAST, 0, HALF, HALF, "reused")
+        quantize(LAST, 0, HALF)
+        quantize(2, 1, HALF, "reused")
+        cast(LAST, 1, HALF, HALF)
+        quantize(LAST, 1, HALF)
+        product(0, 0, [0, 1, 2, 3], "bank_a")
+        fetch(0, 0)
         place(0, 0)
-        cast(2, 1, 0)
-        cast(3, 1, HALF, "first_result")
-        quantize(2, 1)
-        quantize(3, 1)
-        for a in range(2):
-            multiply(a, 0, 1)
-        for a in range(PASSES):
-            multiply(a, 1, 0)
-        for a in range(2):
-            multiply(a, 1, 1)
-        multiply(2, 0, 1)
-        multiply(2, 1, 1)
-        multiply(LAST, 0, 1)
-        multiply(LAST, 1, 1)
-        fetch(1, 0, "last_rows")
+        product(1, 0, [3, 0, 1, 2], "bank_b")
+        fetch(1, 0)
         place(1, 0)
-        for m in range(M_TILES):
-            fetch(m, 1)
-            place(m, 1)
-            store(m)
+        product(0, 1, [2, 0, 1, 3], "bank_c")
+        fetch(0, 1)
+        place(0, 1)
+        store(0)
+        product(1, 1, [2, 0, 1, 3], "bank_d")
+        fetch(1, 1)
+        place(1, 1)
+        store(1)

@@ -62,7 +62,7 @@ def tile_list_hscat_none_kernel(tc, x, w_words, w_scales, wgo, offs, out):
                     words[m, a] = both[:, a - a0, (m - m0) * P : (m - m0 + 1) * P]
 
         def load_scales(q):
-            nc.sync.dma_start(
+            nc.scalar.dma_start(
                 out=packed[32 * q : 32 * q + 16, :].bitcast(I32),
                 in_=w_scales[:, 4 * q : 4 * q + 4, :].bitcast(I32),
             )
@@ -72,18 +72,18 @@ def tile_list_hscat_none_kernel(tc, x, w_words, w_scales, wgo, offs, out):
             for h in range(h0, h1):
                 weights[h] = all_weights[:, h * HALF : (h + 1) * HALF]
 
-        load_x(0, 0, S)
-        for q in range(3):
+        for q in range(4):
             load_scales(q)
+        load_x(0, 0, S)
         load_x(1, 0, S)
         load_x(2, 0, S)
         load_x(LAST, 0, HALF)
         load_w(0, 1, 0, PASSES)
-        load_scales(3)
-        load_w(1, 2, 0, PASSES)
+        load_w(1, 2, 2, PASSES)
         load_x(LAST, 1, HALF)
-        nc.sync.dma_start(offsets[:], offs)
+        load_w(1, 2, 0, 2)
         load_weights(0, HALVES)
+        nc.sync.dma_start(offsets[:], offs)
 
         acc = {}
         results = {}
@@ -155,22 +155,22 @@ def tile_list_hscat_none_kernel(tc, x, w_words, w_scales, wgo, offs, out):
         cast(2, 0, HALF, 88)
         quantize(2, 0, HALF)
         cast(2, 1, HALF, 0)
-        cast(LAST, 0, HALF, HALF, "reused")
+        cast(LAST, 0, HALF, HALF)
         quantize(LAST, 0, HALF)
-        quantize(2, 1, HALF, "reused")
+        quantize(2, 1, HALF)
         cast(LAST, 1, HALF, HALF)
         quantize(LAST, 1, HALF)
         product(0, 0, [0, 1, 2, 3], "bank_a")
         fetch(0, 0)
         place(0, 0)
-        product(1, 0, [3, 0, 1, 2], "bank_b")
+        product(1, 0, [3, 2, 0, 1], "bank_b")
         fetch(1, 0)
         place(1, 0)
-        product(0, 1, [2, 0, 1, 3], "bank_c")
+        product(0, 1, [3, 0, 1, 2], "bank_c")
         fetch(0, 1)
         place(0, 1)
         store(0)
-        product(1, 1, [2, 0, 1, 3], "bank_d")
+        product(1, 1, [3, 0, 1, 2], "bank_d")
         fetch(1, 1)
         place(1, 1)
         store(1)

@@ -79,9 +79,9 @@ def tile_list_hscat_none_kernel(tc, x, w_words, w_scales, wgo, offs, out):
         load_x(2, 0, S)
         load_x(LAST, 0, HALF)
         load_w(0, 1, 0, PASSES)
-        load_w(1, 2, 2, PASSES)
+        load_w(1, 2, LAST, PASSES)
         load_x(LAST, 1, HALF)
-        load_w(1, 2, 0, 2)
+        load_w(1, 2, 0, LAST)
         load_weights(0, HALVES)
         nc.sync.dma_start(offsets[:], offs)
 
@@ -163,7 +163,7 @@ def tile_list_hscat_none_kernel(tc, x, w_words, w_scales, wgo, offs, out):
         product(0, 0, [0, 1, 2, 3], "bank_a")
         fetch(0, 0)
         place(0, 0)
-        product(1, 0, [3, 2, 0, 1], "bank_b")
+        product(1, 0, [3, 0, 1, 2], "bank_b")
         fetch(1, 0)
         place(1, 0)
         product(0, 1, [3, 0, 1, 2], "bank_c")

@@ -36,7 +36,7 @@ def tile_list_hscat_none_kernel(tc, x, w_words, w_scales, wgo, offs, out):
         packed = tile([P, M], U8, "packed")
         windows = [tile([P, T], F32, f"window_{m}") for m in range(M_TILES)]
         for m in range(M_TILES):
-            nc.gpsimd.memset(windows[m][:], 0.0)
+            nc.vector.memset(windows[m][:], 0.0)
 
         offsets = keep.tile([P, S // 16], U16, name="offsets")
         all_weights = tile([P, S], F32, "all_weights")

@@ -76,8 +76,8 @@ def tile_list_hscat_none_kernel(tc, x, w_words, w_scales, wgo, offs, out):
             load_scales(q)
         load_x(0, 0, S)
         load_x(1, 0, S)
-        load_x(2, 0, S)
         load_x(LAST, 0, HALF)
+        load_x(2, 0, S)
         load_w(0, 1, 0, PASSES)
         load_w(1, 2, LAST, PASSES)
         load_x(LAST, 1, HALF)
@@ -152,15 +152,15 @@ def tile_list_hscat_none_kernel(tc, x, w_words, w_scales, wgo, offs, out):
         for a in range(2):
             cast(a, 0, S, 176)
             quantize(a, 0, S)
+        cast(LAST, 0, HALF, HALF)
+        quantize(LAST, 0, HALF)
         cast(2, 0, HALF, 88)
         quantize(2, 0, HALF)
         cast(2, 1, HALF, 0)
-        cast(LAST, 0, HALF, HALF)
-        quantize(LAST, 0, HALF)
         quantize(2, 1, HALF)
         cast(LAST, 1, HALF, HALF)
         quantize(LAST, 1, HALF)
-        product(0, 0, [0, 1, 2, 3], "bank_a")
+        product(0, 0, [0, 1, 3, 2], "bank_a")
         fetch(0, 0)
         place(0, 0)
         product(1, 0, [3, 0, 1, 2], "bank_b")

@@ -78,8 +78,8 @@ def tile_list_hscat_none_kernel(tc, x, w_words, w_scales, wgo, offs, out):
         load_x(1, 0, S)
         load_x(LAST, 0, HALF)
         load_x(2, 0, S)
-        load_w(0, 1, 0, PASSES)
         load_w(1, 2, LAST, PASSES)
+        load_w(0, 1, 0, PASSES)
         load_x(LAST, 1, HALF)
         load_w(1, 2, 0, LAST)
         load_weights(0, HALVES)
@@ -116,6 +116,21 @@ def tile_list_hscat_none_kernel(tc, x, w_words, w_scales, wgo, offs, out):
             for i in range(width // HALF):
                 cols = slice(i * HALF, (i + 1) * HALF)
                 quantized[a, h + i] = (codes[:, cols], scales[:, cols])
+
+        def cast_and_quantize_in_two(a, h):
+            quarter = HALF // 2
+            interleaved[a, h] = tile([P, HALF, PACK], BF16, f"grouped_{a}_{h}")
+            codes = tile([P, HALF], U32, f"codes_{a}_{h}")
+            scales = tile([P, HALF], U8, f"scales_{a}_{h}")
+            for c0 in (0, quarter):
+                interleave(nc.vector.tensor_copy, a, h, c0, c0 + quarter)
+            for c0 in (0, quarter):
+                nc.vector.quantize_mx(
+                    out=codes[:, c0 : c0 + quarter].bitcast(FP8X4),
+                    scales=scales[:, c0 : c0 + quarter],
+                    in_=interleaved[a, h][:, c0 : c0 + quarter, :].rearrange("p w t -> p (w t)"),
+                )
+            quantized[a, h] = (codes[:], scales[:])
 
         def multiply(a, m, h, start, stop):
             codes, scales = quantized[a, h]
@@ -158,8 +173,7 @@ def tile_list_hscat_none_kernel(tc, x, w_words, w_scales, wgo, offs, out):
         quantize(2, 0, HALF)
         cast(2, 1, HALF, 0)
         quantize(2, 1, HALF)
-        cast(LAST, 1, HALF, HALF)
-        quantize(LAST, 1, HALF)
+        cast_and_quantize_in_two(LAST, 1)
         product(0, 0, [0, 1, 3, 2], "bank_a")
         fetch(0, 0)
         place(0, 0)

@@ -31,7 +31,7 @@ def tile_list_hscat_none_kernel(tc, x, w_words, w_scales, wgo, offs, out):
         psum = ctx.enter_context(tc.psum_pool(name="psum", bufs=1))
 
         def tile(shape, dtype, name, tag=None):
-            return keep.tile(shape, dtype, name=name, tag=tag or name, align_bytes=64)
+            return keep.tile(shape, dtype, name=name, tag=tag or name, align_bytes=256)
 
         packed = tile([P, M], U8, "packed")
         windows = [tile([P, T], F32, f"window_{m}") for m in range(M_TILES)]

@@ -78,8 +78,8 @@ def tile_list_hscat_none_kernel(tc, x, w_words, w_scales, wgo, offs, out):
         load_x(1, 0, S)
         load_x(LAST, 0, HALF)
         load_x(2, 0, S)
-        load_w(1, 2, LAST, PASSES)
-        load_w(0, 1, 0, PASSES)
+        load_w(0, 2, LAST, PASSES)
+        load_w(0, 1, 0, LAST)
         load_x(LAST, 1, HALF)
         load_w(1, 2, 0, LAST)
         load_weights(0, HALVES)
@@ -165,16 +165,18 @@ def tile_list_hscat_none_kernel(tc, x, w_words, w_scales, wgo, offs, out):
             nc.sync.dma_start(out=out[m * P : (m + 1) * P, :], in_=windows[m][:])
 
         for a in range(2):
-            cast(a, 0, S, 176)
-            quantize(a, 0, S)
+            cast(a, 0, HALF, HALF)
+            cast(a, 1, HALF, 0)
+            quantize(a, 0, HALF)
+            quantize(a, 1, HALF)
         cast(LAST, 0, HALF, HALF)
         quantize(LAST, 0, HALF)
-        cast(2, 0, HALF, 88)
+        cast(2, 0, HALF, 64)
         quantize(2, 0, HALF)
         cast(2, 1, HALF, 0)
         quantize(2, 1, HALF)
         cast_and_quantize_in_two(LAST, 1)
-        product(0, 0, [0, 1, 3, 2], "bank_a")
+        product(0, 0, [3, 0, 1, 2], "bank_a")
         fetch(0, 0)
         place(0, 0)
         product(1, 0, [3, 0, 1, 2], "bank_b")

@@ -21,7 +21,14 @@ PASSES = K // K_PASS
 HALF = S // 2
 HALVES = S // HALF
 M_TILES = M // P
-LAST = PASSES - 1
+QUADRANT = 32
+SCALE_ROWS = 4
+GROUP = 16
+LIST_COLS = HALF // GROUP
+LINE = 4
+SPLIT = PASSES - 1
+LAST_WHOLE = SPLIT - 1
+ALIGN = 256
 
 
 def tile_list_hscat_none_kernel(tc, x, w_words, w_scales, wgo, offs, out):
@@ -30,163 +37,134 @@ def tile_list_hscat_none_kernel(tc, x, w_words, w_scales, wgo, offs, out):
         keep = ctx.enter_context(tc.tile_pool(name="keep", bufs=1))
         psum = ctx.enter_context(tc.psum_pool(name="psum", bufs=1))
 
-        def tile(shape, dtype, name, tag=None):
-            return keep.tile(shape, dtype, name=name, tag=tag or name, align_bytes=256)
+        def tile(shape, dtype, name):
+            return keep.tile(shape, dtype, name=name, tag=name, align_bytes=ALIGN)
 
-        packed = tile([P, M], U8, "packed")
+        w_scale_rows = tile([P, M], U8, "w_scale_rows")
+
         windows = [tile([P, T], F32, f"window_{m}") for m in range(M_TILES)]
         for m in range(M_TILES):
             nc.vector.memset(windows[m][:], 0.0)
 
-        offsets = keep.tile([P, S // 16], U16, name="offsets")
-        all_weights = tile([P, S], F32, "all_weights")
-        weights = {}
-        words = {}
-        raw = {}
+        offsets = keep.tile([P, S // GROUP], U16, name="offsets")
+        weights = tile([P, S], F32, "weights")
+        x_rows = {}
+        w_codes = {}
 
-        def load_x(a, h, width, tag=None):
-            loaded = tile([P, PACK, width], F32, f"raw_{a}_{h}", tag)
-            rows = x[a * K_PASS : (a + 1) * K_PASS, h * HALF : h * HALF + width]
-            nc.sync.dma_start(out=loaded[:], in_=rows.rearrange("(p j) w -> p j w", j=PACK))
-            for i in range(width // HALF):
-                raw[a, h + i] = loaded[:, :, i * HALF :]
+        def load_scales(q):
+            nc.scalar.dma_start(
+                out=w_scale_rows[QUADRANT * q : QUADRANT * q + PASSES * SCALE_ROWS, :].bitcast(I32),
+                in_=w_scales[:, SCALE_ROWS * q : SCALE_ROWS * (q + 1), :].bitcast(I32),
+            )
+
+        def load_x(a, h0, h1):
+            loaded = tile([P, PACK, (h1 - h0) * HALF], F32, f"x_rows_{a}_{h0}")
+            rows = x[a * K_PASS : (a + 1) * K_PASS, h0 * HALF : h1 * HALF]
+            nc.sync.dma_start(out=loaded[:], in_=rows.rearrange("(p t) j -> p t j", t=PACK))
+            for h in range(h0, h1):
+                x_rows[a, h] = loaded[:, :, (h - h0) * HALF : (h - h0 + 1) * HALF]
 
         def load_w(m0, m1, a0, a1):
-            both = tile([P, a1 - a0, (m1 - m0) * P], U32, f"words_{m0}_{a0}")
+            loaded = tile([P, a1 - a0, (m1 - m0) * P], U32, f"w_codes_{m0}_{a0}")
             nc.sync.dma_start(
-                out=both[:].bitcast(I32),
+                out=loaded[:].bitcast(I32),
                 in_=w_words[a0:a1, :, m0 * P : m1 * P, :].rearrange("a p n t -> p a (n t)").bitcast(I32),
             )
             for m in range(m0, m1):
                 for a in range(a0, a1):
-                    words[m, a] = both[:, a - a0, (m - m0) * P : (m - m0 + 1) * P]
+                    w_codes[m, a] = loaded[:, a - a0, (m - m0) * P : (m - m0 + 1) * P]
 
-        def load_scales(q):
-            nc.scalar.dma_start(
-                out=packed[32 * q : 32 * q + 16, :].bitcast(I32),
-                in_=w_scales[:, 4 * q : 4 * q + 4, :].bitcast(I32),
-            )
-
-        def load_weights(h0, h1):
-            nc.sync.dma_start(out=all_weights[:, h0 * HALF : h1 * HALF], in_=wgo[:, h0 * HALF : h1 * HALF])
-            for h in range(h0, h1):
-                weights[h] = all_weights[:, h * HALF : (h + 1) * HALF]
-
-        for q in range(4):
+        for q in range(P // QUADRANT):
             load_scales(q)
-        load_x(0, 0, S)
-        load_x(1, 0, S)
-        load_x(LAST, 0, HALF)
-        load_x(2, 0, S)
-        load_w(0, 2, LAST, PASSES)
-        load_w(0, 1, 0, LAST)
-        load_x(LAST, 1, HALF)
-        load_w(1, 2, 0, LAST)
-        load_weights(0, HALVES)
+        for a in range(LAST_WHOLE):
+            load_x(a, 0, HALVES)
+        load_x(SPLIT, 0, 1)
+        load_x(LAST_WHOLE, 0, HALVES)
+        load_w(0, M_TILES, SPLIT, PASSES)
+        load_w(0, 1, 0, SPLIT)
+        load_x(SPLIT, 1, HALVES)
+        load_w(1, M_TILES, 0, SPLIT)
+        nc.sync.dma_start(out=weights[:], in_=wgo)
         nc.sync.dma_start(offsets[:], offs)
 
-        acc = {}
-        results = {}
-        interleaved = {}
-        quantized = {}
+        rounded = {}
+        x_codes = {}
+        x_scales = {}
+        whole = [(0, HALF)]
+        in_two = [(0, HALF // 2), (HALF // 2, HALF)]
 
-        def interleave(copy, a, h, c0, c1):
-            copy(
-                out=interleaved[a, h][:, c0:c1, :].rearrange("p (c i) t -> p c t i", i=4),
-                in_=raw[a, h][:, :, c0:c1].rearrange("p t (c i) -> p c t i", i=4),
-            )
+        def new_rounded(a, h):
+            rounded[a, h] = tile([P, HALF, PACK], BF16, f"rounded_{a}_{h}")
 
-        def cast(a, h, width, vector_cols, tag=None):
-            interleaved[a, h] = tile([P, width, PACK], BF16, f"grouped_{a}_{h}", tag)
-            if vector_cols > 0:
-                interleave(nc.vector.tensor_copy, a, h, 0, vector_cols)
-            if vector_cols < width:
-                interleave(nc.scalar.copy, a, h, vector_cols, width)
+        def new_quantized(a, h):
+            x_codes[a, h] = tile([P, HALF], U32, f"x_codes_{a}_{h}")
+            x_scales[a, h] = tile([P, HALF], U8, f"x_scales_{a}_{h}")
 
-        def quantize(a, h, width, tag=None):
-            codes = tile([P, width], U32, f"codes_{a}_{h}", tag)
-            scales = tile([P, width], U8, f"scales_{a}_{h}")
-            whole = (a, h) if (a, h) in interleaved else (a, 0)
-            c0 = (h - whole[1]) * HALF
-            nc.vector.quantize_mx(
-                out=codes[:].bitcast(FP8X4),
-                scales=scales[:],
-                in_=interleaved[whole][:, c0 : c0 + width, :].rearrange("p w t -> p (w t)"),
-            )
-            for i in range(width // HALF):
-                cols = slice(i * HALF, (i + 1) * HALF)
-                quantized[a, h + i] = (codes[:, cols], scales[:, cols])
-
-        def cast_and_quantize_in_two(a, h):
-            quarter = HALF // 2
-            interleaved[a, h] = tile([P, HALF, PACK], BF16, f"grouped_{a}_{h}")
-            codes = tile([P, HALF], U32, f"codes_{a}_{h}")
-            scales = tile([P, HALF], U8, f"scales_{a}_{h}")
-            for c0 in (0, quarter):
-                interleave(nc.vector.tensor_copy, a, h, c0, c0 + quarter)
-            for c0 in (0, quarter):
-                nc.vector.quantize_mx(
-                    out=codes[:, c0 : c0 + quarter].bitcast(FP8X4),
-                    scales=scales[:, c0 : c0 + quarter],
-                    in_=interleaved[a, h][:, c0 : c0 + quarter, :].rearrange("p w t -> p (w t)"),
+        def round_parts(a, h, copies, parts):
+            for copy, (c0, c1) in zip(copies, parts):
+                copy(
+                    out=rounded[a, h][:, c0:c1, :].rearrange("p (c i) t -> p c t i", i=LINE),
+                    in_=x_rows[a, h][:, :, c0:c1].rearrange("p t (c i) -> p c t i", i=LINE),
                 )
-            quantized[a, h] = (codes[:], scales[:])
 
-        def multiply(a, m, h, start, stop):
-            codes, scales = quantized[a, h]
-            nc.tensor.matmul_mx(
-                out=acc[m, h][:],
-                lhsT=words[m, a].bitcast(FP8X4),
-                lhsT_scale=packed[4 * a :, m * P : (m + 1) * P],
-                rhs=codes.bitcast(FP8X4),
-                rhs_scale=scales,
-                start=start,
-                stop=stop,
-            )
+        def quantize_parts(a, h, parts):
+            for c0, c1 in parts:
+                nc.vector.quantize_mx(
+                    out=x_codes[a, h][:, c0:c1].bitcast(FP8X4),
+                    scales=x_scales[a, h][:, c0:c1],
+                    in_=rounded[a, h][:, c0:c1, :].rearrange("p j t -> p (j t)"),
+                )
 
-        def product(m, h, order, bank):
-            acc[m, h] = psum.tile([P, HALF], F32, name=f"acc_{m}_{h}", tag=bank)
-            for a in order:
-                multiply(a, m, h, a == order[0], a == order[-1])
+        def round_half(a, h, copies, parts):
+            new_rounded(a, h)
+            round_parts(a, h, copies, parts)
 
-        def fetch(m, h, tag=None):
-            results[m, h] = tile([P, HALF], F32, f"y_{m}_{h}", tag)
-            nc.scalar.copy(out=results[m, h][:], in_=acc[m, h][:])
+        def quantize_half(a, h):
+            new_quantized(a, h)
+            quantize_parts(a, h, whole)
 
-        def place(m, h):
-            nc.vector.tensor_tensor(
-                windows[m][:].indirect(offsets[:, 8 * h : 8 * h + 8]),
-                results[m, h][:],
-                weights[h],
-                MULT,
-            )
+        on_vector = nc.vector.tensor_copy
+        on_scalar = nc.scalar.copy
 
-        def store(m):
-            nc.sync.dma_start(out=out[m * P : (m + 1) * P, :], in_=windows[m][:])
+        for a in range(LAST_WHOLE):
+            round_half(a, 0, [on_vector], whole)
+            round_half(a, 1, [on_scalar], whole)
+            for h in range(HALVES):
+                quantize_half(a, h)
+        round_half(SPLIT, 0, [on_vector], whole)
+        quantize_half(SPLIT, 0)
 
-        for a in range(2):
-            cast(a, 0, HALF, HALF)
-            cast(a, 1, HALF, 0)
-            quantize(a, 0, HALF)
-            quantize(a, 1, HALF)
-        cast(LAST, 0, HALF, HALF)
-        quantize(LAST, 0, HALF)
-        cast(2, 0, HALF, 64)
-        quantize(2, 0, HALF)
-        cast(2, 1, HALF, 0)
-        quantize(2, 1, HALF)
-        cast_and_quantize_in_two(LAST, 1)
-        product(0, 0, [3, 0, 1, 2], "bank_a")
-        fetch(0, 0)
-        place(0, 0)
-        product(1, 0, [3, 0, 1, 2], "bank_b")
-        fetch(1, 0)
-        place(1, 0)
-        product(0, 1, [3, 0, 1, 2], "bank_c")
-        fetch(0, 1)
-        place(0, 1)
-        store(0)
-        product(1, 1, [3, 0, 1, 2], "bank_d")
-        fetch(1, 1)
-        place(1, 1)
-        store(1)
+        round_half(LAST_WHOLE, 0, [on_vector, on_scalar], in_two)
+        quantize_half(LAST_WHOLE, 0)
+        round_half(LAST_WHOLE, 1, [on_scalar], whole)
+        quantize_half(LAST_WHOLE, 1)
+
+        new_rounded(SPLIT, 1)
+        new_quantized(SPLIT, 1)
+        round_parts(SPLIT, 1, [on_vector, on_vector], in_two)
+        quantize_parts(SPLIT, 1, in_two)
+
+        order = [SPLIT, *range(SPLIT)]
+        for h in range(HALVES):
+            for m in range(M_TILES):
+                total = psum.tile([P, HALF], F32, name=f"total_{m}_{h}", tag=f"bank_{m}_{h}")
+                for a in order:
+                    nc.tensor.matmul_mx(
+                        out=total[:],
+                        lhsT=w_codes[m, a].bitcast(FP8X4),
+                        lhsT_scale=w_scale_rows[SCALE_ROWS * a :, m * P : (m + 1) * P],
+                        rhs=x_codes[a, h][:].bitcast(FP8X4),
+                        rhs_scale=x_scales[a, h][:],
+                        start=a == order[0],
+                        stop=a == order[-1],
+                    )
+                y = tile([P, HALF], F32, f"y_{m}_{h}")
+                nc.scalar.copy(out=y[:], in_=total[:])
+                nc.vector.tensor_tensor(
+                    windows[m][:].indirect(offsets[:, LIST_COLS * h : LIST_COLS * (h + 1)]),
+                    y[:],
+                    weights[:, h * HALF : (h + 1) * HALF],
+                    MULT,
+                )
+                if h == HALVES - 1:
+                    nc.sync.dma_start(out=out[m * P : (m + 1) * P, :], in_=windows[m][:])

@@ -76,9 +76,9 @@ def tile_list_hscat_none_kernel(tc, x, w_words, w_scales, wgo, offs, out):
 
         for q in range(P // QUADRANT):
             load_scales(q)
+        load_x(SPLIT, 0, 1)
         for a in range(LAST_WHOLE):
             load_x(a, 0, HALVES)
-        load_x(SPLIT, 0, 1)
         load_x(LAST_WHOLE, 0, HALVES)
         load_w(0, M_TILES, SPLIT, PASSES)
         load_w(0, 1, 0, SPLIT)
@@ -126,13 +126,13 @@ def tile_list_hscat_none_kernel(tc, x, w_words, w_scales, wgo, offs, out):
         on_vector = nc.vector.tensor_copy
         on_scalar = nc.scalar.copy
 
+        round_half(SPLIT, 0, [on_vector], whole)
+        quantize_half(SPLIT, 0)
         for a in range(LAST_WHOLE):
             round_half(a, 0, [on_vector], whole)
             round_half(a, 1, [on_scalar], whole)
             for h in range(HALVES):
                 quantize_half(a, h)
-        round_half(SPLIT, 0, [on_vector], whole)
-        quantize_half(SPLIT, 0)
 
         round_half(LAST_WHOLE, 0, [on_vector, on_scalar], in_two)
         quantize_half(LAST_WHOLE, 0)

@@ -26,8 +26,6 @@ SCALE_ROWS = 4
 GROUP = 16
 LIST_COLS = HALF // GROUP
 LINE = 4
-SPLIT = PASSES - 1
-LAST_WHOLE = SPLIT - 1
 ALIGN = 256
 
 
@@ -37,36 +35,55 @@ def tile_list_hscat_none_kernel(tc, x, w_words, w_scales, wgo, offs, out):
         keep = ctx.enter_context(tc.tile_pool(name="keep", bufs=1))
         psum = ctx.enter_context(tc.psum_pool(name="psum", bufs=1))
 
-        def tile(shape, dtype, name):
-            return keep.tile(shape, dtype, name=name, tag=name, align_bytes=ALIGN)
+        def tile(shape, dtype, name, tag=None):
+            return keep.tile(shape, dtype, name=name, tag=tag or name, align_bytes=4096 if name.startswith("x_rows") or name.startswith("window") else ALIGN)
 
         w_scale_rows = tile([P, M], U8, "w_scale_rows")
-
         windows = [tile([P, T], F32, f"window_{m}") for m in range(M_TILES)]
         for m in range(M_TILES):
             nc.vector.memset(windows[m][:], 0.0)
 
-        offsets = keep.tile([P, S // GROUP], U16, name="offsets")
-        weights = tile([P, S], F32, "weights")
+        offsets = tile([P, S // GROUP], U16, "offsets")
         x_rows = {}
         w_codes = {}
+        weights = {}
+        rounded = {}
+        x_codes = {}
+        x_scales = {}
+        totals = {}
+        passes_done = {}
+        results = {}
+        on_vector = nc.vector.tensor_copy
+        on_scalar = nc.scalar.copy
 
-        def load_scales(q):
-            nc.scalar.dma_start(
-                out=w_scale_rows[QUADRANT * q : QUADRANT * q + PASSES * SCALE_ROWS, :].bitcast(I32),
-                in_=w_scales[:, SCALE_ROWS * q : SCALE_ROWS * (q + 1), :].bitcast(I32),
-            )
+        def load_scales(queue=nc.scalar):
+            for q in range(P // QUADRANT):
+                queue.dma_start(
+                    out=w_scale_rows[QUADRANT * q : QUADRANT * q + PASSES * SCALE_ROWS, :].bitcast(I32),
+                    in_=w_scales[:, SCALE_ROWS * q : SCALE_ROWS * (q + 1), :].bitcast(I32),
+                )
 
-        def load_x(a, h0, h1):
+        def load_x(a, h0, h1, queue=nc.sync):
             loaded = tile([P, PACK, (h1 - h0) * HALF], F32, f"x_rows_{a}_{h0}")
             rows = x[a * K_PASS : (a + 1) * K_PASS, h0 * HALF : h1 * HALF]
-            nc.sync.dma_start(out=loaded[:], in_=rows.rearrange("(p t) j -> p t j", t=PACK))
+            queue.dma_start(out=loaded[:], in_=rows.rearrange("(p t) j -> p t j", t=PACK))
             for h in range(h0, h1):
                 x_rows[a, h] = loaded[:, :, (h - h0) * HALF : (h - h0 + 1) * HALF]
 
-        def load_w(m0, m1, a0, a1):
-            loaded = tile([P, a1 - a0, (m1 - m0) * P], U32, f"w_codes_{m0}_{a0}")
+        def load_x_pair(a):
+            loaded = tile([P, 2, PACK, S], F32, f"x_rows_{a}_0")
+            rows = x[a * K_PASS : (a + 2) * K_PASS, :]
             nc.sync.dma_start(
+                out=loaded[:].rearrange("p b t j -> p b (t j)"),
+                in_=rows.rearrange("(b p t) j -> p b (t j)", b=2, t=PACK),
+            )
+            for b in range(2):
+                for h in range(HALVES):
+                    x_rows[a + b, h] = loaded[:, b, :, h * HALF : (h + 1) * HALF]
+
+        def load_w(m0, m1, a0, a1, queue=nc.sync, tag=None):
+            loaded = tile([P, a1 - a0, (m1 - m0) * P], U32, f"w_codes_{m0}_{a0}", tag)
+            queue.dma_start(
                 out=loaded[:].bitcast(I32),
                 in_=w_words[a0:a1, :, m0 * P : m1 * P, :].rearrange("a p n t -> p a (n t)").bitcast(I32),
             )
@@ -74,97 +91,99 @@ def tile_list_hscat_none_kernel(tc, x, w_words, w_scales, wgo, offs, out):
                 for a in range(a0, a1):
                     w_codes[m, a] = loaded[:, a - a0, (m - m0) * P : (m - m0 + 1) * P]
 
-        for q in range(P // QUADRANT):
-            load_scales(q)
-        load_x(SPLIT, 0, 1)
-        for a in range(LAST_WHOLE):
-            load_x(a, 0, HALVES)
-        load_x(LAST_WHOLE, 0, HALVES)
-        load_w(0, M_TILES, SPLIT, PASSES)
-        load_w(0, 1, 0, SPLIT)
-        load_x(SPLIT, 1, HALVES)
-        load_w(1, M_TILES, 0, SPLIT)
-        nc.sync.dma_start(out=weights[:], in_=wgo)
-        nc.sync.dma_start(offsets[:], offs)
+        def load_weights(h0, h1, queue=nc.sync):
+            loaded = tile([P, (h1 - h0) * HALF], F32, f"weights_{h0}")
+            queue.dma_start(out=loaded[:], in_=wgo[:, h0 * HALF : h1 * HALF])
+            for h in range(h0, h1):
+                weights[h] = loaded[:, (h - h0) * HALF : (h - h0 + 1) * HALF]
 
-        rounded = {}
-        x_codes = {}
-        x_scales = {}
-        whole = [(0, HALF)]
-        in_two = [(0, HALF // 2), (HALF // 2, HALF)]
+        def load_lists():
+            nc.sync.dma_start(offsets[:], offs)
 
-        def new_rounded(a, h):
-            rounded[a, h] = tile([P, HALF, PACK], BF16, f"rounded_{a}_{h}")
+        def round_cols(a, h, copy, c0, c1, tag=None):
+            if (a, h) not in rounded:
+                rounded[a, h] = tile([P, HALF, PACK], BF16, f"rounded_{a}_{h}", tag)
+            copy(
+                out=rounded[a, h][:, c0:c1, :].rearrange("p (c i) t -> p c t i", i=LINE),
+                in_=x_rows[a, h][:, :, c0:c1].rearrange("p t (c i) -> p c t i", i=LINE),
+            )
 
-        def new_quantized(a, h):
-            x_codes[a, h] = tile([P, HALF], U32, f"x_codes_{a}_{h}")
-            x_scales[a, h] = tile([P, HALF], U8, f"x_scales_{a}_{h}")
+        def round_shared(a, h, on_v=HALF // 2):
+            round_cols(a, h, on_vector, 0, on_v)
+            round_cols(a, h, on_scalar, on_v, HALF)
 
-        def round_parts(a, h, copies, parts):
-            for copy, (c0, c1) in zip(copies, parts):
-                copy(
-                    out=rounded[a, h][:, c0:c1, :].rearrange("p (c i) t -> p c t i", i=LINE),
-                    in_=x_rows[a, h][:, :, c0:c1].rearrange("p t (c i) -> p c t i", i=LINE),
+        def quantize(a, h, c0=0, c1=HALF):
+            if (a, h) not in x_codes:
+                x_codes[a, h] = tile([P, HALF], U32, f"x_codes_{a}_{h}")
+                x_scales[a, h] = tile([P, HALF], U8, f"x_scales_{a}_{h}")
+            nc.vector.quantize_mx(
+                out=x_codes[a, h][:, c0:c1].bitcast(FP8X4),
+                scales=x_scales[a, h][:, c0:c1],
+                in_=rounded[a, h][:, c0:c1, :].rearrange("p j t -> p (j t)"),
+            )
+
+        def multiply(m, h, passes):
+            if (m, h) not in totals:
+                totals[m, h] = psum.tile([P, HALF], F32, name=f"total_{m}_{h}", tag=f"bank_{m}_{h}")
+                passes_done[m, h] = []
+            for a in passes:
+                passes_done[m, h].append(a)
+                nc.tensor.matmul_mx(
+                    out=totals[m, h][:],
+                    lhsT=w_codes[m, a].bitcast(FP8X4),
+                    lhsT_scale=w_scale_rows[SCALE_ROWS * a :, m * P : (m + 1) * P],
+                    rhs=x_codes[a, h][:].bitcast(FP8X4),
+                    rhs_scale=x_scales[a, h][:],
+                    start=len(passes_done[m, h]) == 1,
+                    stop=len(passes_done[m, h]) == PASSES,
                 )
 
-        def quantize_parts(a, h, parts):
-            for c0, c1 in parts:
-                nc.vector.quantize_mx(
-                    out=x_codes[a, h][:, c0:c1].bitcast(FP8X4),
-                    scales=x_scales[a, h][:, c0:c1],
-                    in_=rounded[a, h][:, c0:c1, :].rearrange("p j t -> p (j t)"),
-                )
+        def leave_psum(m, h, copy=on_scalar, tag=None):
+            results[m, h] = tile([P, HALF], F32, f"y_{m}_{h}", tag)
+            copy(out=results[m, h][:], in_=totals[m, h][:])
 
-        def round_half(a, h, copies, parts):
-            new_rounded(a, h)
-            round_parts(a, h, copies, parts)
+        def scatter(m, h):
+            nc.vector.tensor_tensor(
+                windows[m][:].indirect(offsets[:, LIST_COLS * h : LIST_COLS * (h + 1)]),
+                weights[h],
+                results[m, h][:],
+                MULT,
+            )
 
-        def quantize_half(a, h):
-            new_quantized(a, h)
-            quantize_parts(a, h, whole)
+        def store(m, queue=nc.sync):
+            queue.dma_start(out=out[m * P : (m + 1) * P, :], in_=windows[m][:])
 
-        on_vector = nc.vector.tensor_copy
-        on_scalar = nc.scalar.copy
+        load_scales()
+        load_x(3, 0, 1)
+        load_x(0, 0, 2)
+        load_x(1, 0, 2)
+        load_x(2, 0, 2)
+        load_w(0, 2, 3, 4)
+        load_w(0, 1, 0, 3)
+        load_x(3, 1, 2)
+        load_w(1, 2, 0, 3)
+        load_weights(0, 2)
+        load_lists()
 
-        round_half(SPLIT, 0, [on_vector], whole)
-        quantize_half(SPLIT, 0)
-        for a in range(LAST_WHOLE):
-            round_half(a, 0, [on_vector], whole)
-            round_half(a, 1, [on_scalar], whole)
-            for h in range(HALVES):
-                quantize_half(a, h)
-
-        round_half(LAST_WHOLE, 0, [on_vector, on_scalar], in_two)
-        quantize_half(LAST_WHOLE, 0)
-        round_half(LAST_WHOLE, 1, [on_scalar], whole)
-        quantize_half(LAST_WHOLE, 1)
-
-        new_rounded(SPLIT, 1)
-        new_quantized(SPLIT, 1)
-        round_parts(SPLIT, 1, [on_vector, on_vector], in_two)
-        quantize_parts(SPLIT, 1, in_two)
-
-        order = [SPLIT, *range(SPLIT)]
+        round_cols(3, 0, on_vector, 0, HALF)
+        quantize(3, 0)
+        for a in range(2):
+            round_cols(a, 0, on_vector, 0, HALF)
+            round_cols(a, 1, on_scalar, 0, HALF)
+            quantize(a, 0)
+            quantize(a, 1)
+        round_shared(2, 0)
+        quantize(2, 0)
+        round_cols(2, 1, on_scalar, 0, HALF)
+        quantize(2, 1)
+        round_cols(3, 1, on_vector, 0, 64)
+        round_cols(3, 1, on_vector, 64, 128)
+        quantize(3, 1, 0, 64)
+        quantize(3, 1, 64, 128)
         for h in range(HALVES):
             for m in range(M_TILES):
-                total = psum.tile([P, HALF], F32, name=f"total_{m}_{h}", tag=f"bank_{m}_{h}")
-                for a in order:
-                    nc.tensor.matmul_mx(
-                        out=total[:],
-                        lhsT=w_codes[m, a].bitcast(FP8X4),
-                        lhsT_scale=w_scale_rows[SCALE_ROWS * a :, m * P : (m + 1) * P],
-                        rhs=x_codes[a, h][:].bitcast(FP8X4),
-                        rhs_scale=x_scales[a, h][:],
-                        start=a == order[0],
-                        stop=a == order[-1],
-                    )
-                y = tile([P, HALF], F32, f"y_{m}_{h}")
-                nc.scalar.copy(out=y[:], in_=total[:])
-                nc.vector.tensor_tensor(
-                    windows[m][:].indirect(offsets[:, LIST_COLS * h : LIST_COLS * (h + 1)]),
-                    y[:],
-                    weights[:, h * HALF : (h + 1) * HALF],
-                    MULT,
-                )
-                if h == HALVES - 1:
-                    nc.sync.dma_start(out=out[m * P : (m + 1) * P, :], in_=windows[m][:])
+                multiply(m, h, [3, 0, 1, 2])
+                leave_psum(m, h)
+                scatter(m, h)
+                if h == 1:
+                    store(m)

@@ -36,7 +36,7 @@ def tile_list_hscat_none_kernel(tc, x, w_words, w_scales, wgo, offs, out):
         psum = ctx.enter_context(tc.psum_pool(name="psum", bufs=1))
 
         def tile(shape, dtype, name, tag=None):
-            return keep.tile(shape, dtype, name=name, tag=tag or name, align_bytes=4096 if name.startswith("x_rows") or name.startswith("window") else ALIGN)
+            return keep.tile(shape, dtype, name=name, tag=tag or name, align_bytes=ALIGN)
 
         w_scale_rows = tile([P, M], U8, "w_scale_rows")
         windows = [tile([P, T], F32, f"window_{m}") for m in range(M_TILES)]
@@ -56,8 +56,8 @@ def tile_list_hscat_none_kernel(tc, x, w_words, w_scales, wgo, offs, out):
         on_vector = nc.vector.tensor_copy
         on_scalar = nc.scalar.copy
 
-        def load_scales(queue=nc.scalar):
-            for q in range(P // QUADRANT):
+        def load_scales(queue=nc.scalar, quadrants=range(P // QUADRANT)):
+            for q in quadrants:
                 queue.dma_start(
                     out=w_scale_rows[QUADRANT * q : QUADRANT * q + PASSES * SCALE_ROWS, :].bitcast(I32),
                     in_=w_scales[:, SCALE_ROWS * q : SCALE_ROWS * (q + 1), :].bitcast(I32),
@@ -145,35 +145,38 @@ def tile_list_hscat_none_kernel(tc, x, w_words, w_scales, wgo, offs, out):
         def scatter(m, h):
             nc.vector.tensor_tensor(
                 windows[m][:].indirect(offsets[:, LIST_COLS * h : LIST_COLS * (h + 1)]),
-                weights[h],
                 results[m, h][:],
+                weights[h],
                 MULT,
             )
 
         def store(m, queue=nc.sync):
             queue.dma_start(out=out[m * P : (m + 1) * P, :], in_=windows[m][:])
 
-        load_scales()
+        load_scales(nc.scalar, [1, 2, 3])
         load_x(3, 0, 1)
-        load_x(0, 0, 2)
-        load_x(1, 0, 2)
+        load_scales(nc.sync, [0])
+        load_x_pair(0)
         load_x(2, 0, 2)
         load_w(0, 2, 3, 4)
         load_w(0, 1, 0, 3)
         load_x(3, 1, 2)
         load_w(1, 2, 0, 3)
-        load_weights(0, 2)
+        load_weights(0, 1)
         load_lists()
+        load_weights(1, 2)
 
-        round_cols(3, 0, on_vector, 0, HALF)
+        round_shared(3, 0)
         quantize(3, 0)
         for a in range(2):
             round_cols(a, 0, on_vector, 0, HALF)
             round_cols(a, 1, on_scalar, 0, HALF)
+        for a in range(2):
             quantize(a, 0)
-            quantize(a, 1)
-        round_shared(2, 0)
+        round_cols(2, 0, on_vector, 0, HALF)
+        quantize(0, 1)
         quantize(2, 0)
+        quantize(1, 1)
         round_cols(2, 1, on_scalar, 0, HALF)
         quantize(2, 1)
         round_cols(3, 1, on_vector, 0, 64)

@@ -154,9 +154,9 @@ def tile_list_hscat_none_kernel(tc, x, w_words, w_scales, wgo, offs, out):
             queue.dma_start(out=out[m * P : (m + 1) * P, :], in_=windows[m][:])
 
         load_scales(nc.scalar, [1, 2, 3])
-        load_x(3, 0, 1)
-        load_scales(nc.sync, [0])
         load_x_pair(0)
+        load_scales(nc.sync, [0])
+        load_x(3, 0, 1)
         load_x(2, 0, 2)
         load_w(0, 2, 3, 4)
         load_w(0, 1, 0, 3)
@@ -166,17 +166,17 @@ def tile_list_hscat_none_kernel(tc, x, w_words, w_scales, wgo, offs, out):
         load_lists()
         load_weights(1, 2)
 
-        round_shared(3, 0)
-        quantize(3, 0)
         for a in range(2):
             round_cols(a, 0, on_vector, 0, HALF)
             round_cols(a, 1, on_scalar, 0, HALF)
         for a in range(2):
             quantize(a, 0)
-        round_cols(2, 0, on_vector, 0, HALF)
+        round_cols(3, 0, on_vector, 0, HALF)
         quantize(0, 1)
-        quantize(2, 0)
+        quantize(3, 0)
+        round_shared(2, 0)
         quantize(1, 1)
+        quantize(2, 0)
         round_cols(2, 1, on_scalar, 0, HALF)
         quantize(2, 1)
         round_cols(3, 1, on_vector, 0, 64)

@@ -174,7 +174,7 @@ def tile_list_hscat_none_kernel(tc, x, w_words, w_scales, wgo, offs, out):
         round_cols(3, 0, on_vector, 0, HALF)
         quantize(0, 1)
         quantize(3, 0)
-        round_shared(2, 0)
+        round_shared(2, 0, 96)
         quantize(1, 1)
         quantize(2, 0)
         round_cols(2, 1, on_scalar, 0, HALF)

@@ -153,15 +153,28 @@ def tile_list_hscat_none_kernel(tc, x, w_words, w_scales, wgo, offs, out):
         def store(m, queue=nc.sync):
             queue.dma_start(out=out[m * P : (m + 1) * P, :], in_=windows[m][:])
 
+        def warm_up():
+            spare = psum.tile([32, HALF], F32, name="spare", tag="bank_spare")
+            for i in range(6):
+                nc.tensor.matmul_mx(
+                    out=spare[:],
+                    lhsT=x_codes[1, 0][:, 0:32].bitcast(FP8X4),
+                    lhsT_scale=w_scale_rows[:, 0:32],
+                    rhs=x_codes[1, 0][:].bitcast(FP8X4),
+                    rhs_scale=x_scales[1, 0][:],
+                    start=True,
+                    stop=True,
+                )
+
         load_scales(nc.scalar, [1, 2, 3])
         load_x_pair(0)
         load_scales(nc.sync, [0])
         load_x(3, 0, 1)
         load_x(2, 0, 2)
-        load_w(0, 2, 3, 4)
-        load_w(0, 1, 0, 3)
+        load_w(0, 1, 0, 2)
+        load_w(0, 1, 2, 4)
         load_x(3, 1, 2)
-        load_w(1, 2, 0, 3)
+        load_w(1, 2, 0, 4)
         load_weights(0, 1)
         load_lists()
         load_weights(1, 2)
@@ -171,6 +184,7 @@ def tile_list_hscat_none_kernel(tc, x, w_words, w_scales, wgo, offs, out):
             round_cols(a, 1, on_scalar, 0, HALF)
         for a in range(2):
             quantize(a, 0)
+        warm_up()
         round_cols(3, 0, on_vector, 0, HALF)
         quantize(0, 1)
         quantize(3, 0)
@@ -185,7 +199,7 @@ def tile_list_hscat_none_kernel(tc, x, w_words, w_scales, wgo, offs, out):
         quantize(3, 1, 64, 128)
         for h in range(HALVES):
             for m in range(M_TILES):
-                multiply(m, h, [3, 0, 1, 2])
+                multiply(m, h, [3, 0, 1, 2] if h else [0, 1, 3, 2])
                 leave_psum(m, h)
                 scatter(m, h)
                 if h == 1:

@@ -158,10 +158,10 @@ def tile_list_hscat_none_kernel(tc, x, w_words, w_scales, wgo, offs, out):
             for i in range(6):
                 nc.tensor.matmul_mx(
                     out=spare[:],
-                    lhsT=x_codes[1, 0][:, 0:32].bitcast(FP8X4),
+                    lhsT=x_codes[0, 0][:, 0:32].bitcast(FP8X4),
                     lhsT_scale=w_scale_rows[:, 0:32],
-                    rhs=x_codes[1, 0][:].bitcast(FP8X4),
-                    rhs_scale=x_scales[1, 0][:],
+                    rhs=x_codes[0, 0][:].bitcast(FP8X4),
+                    rhs_scale=x_scales[0, 0][:],
                     start=True,
                     stop=True,
                 )
@@ -185,11 +185,11 @@ def tile_list_hscat_none_kernel(tc, x, w_words, w_scales, wgo, offs, out):
         for a in range(2):
             quantize(a, 0)
         warm_up()
-        round_cols(3, 0, on_vector, 0, HALF)
+        round_cols(3, 0, on_scalar, 0, HALF)
         quantize(0, 1)
-        quantize(3, 0)
-        round_shared(2, 0, 96)
         quantize(1, 1)
+        round_shared(2, 0, 96)
+        quantize(3, 0)
         quantize(2, 0)
         round_cols(2, 1, on_scalar, 0, HALF)
         quantize(2, 1)

@@ -158,10 +158,10 @@ def tile_list_hscat_none_kernel(tc, x, w_words, w_scales, wgo, offs, out):
             for i in range(6):
                 nc.tensor.matmul_mx(
                     out=spare[:],
-                    lhsT=x_codes[0, 0][:, 0:32].bitcast(FP8X4),
+                    lhsT=x_codes[0, 1][:, 0:32].bitcast(FP8X4),
                     lhsT_scale=w_scale_rows[:, 0:32],
-                    rhs=x_codes[0, 0][:].bitcast(FP8X4),
-                    rhs_scale=x_scales[0, 0][:],
+                    rhs=x_codes[0, 1][:].bitcast(FP8X4),
+                    rhs_scale=x_scales[0, 1][:],
                     start=True,
                     stop=True,
                 )
@@ -184,9 +184,9 @@ def tile_list_hscat_none_kernel(tc, x, w_words, w_scales, wgo, offs, out):
             round_cols(a, 1, on_scalar, 0, HALF)
         for a in range(2):
             quantize(a, 0)
-        warm_up()
         round_cols(3, 0, on_scalar, 0, HALF)
         quantize(0, 1)
+        warm_up()
         quantize(1, 1)
         round_shared(2, 0, 96)
         quantize(3, 0)
@@ -199,7 +199,7 @@ def tile_list_hscat_none_kernel(tc, x, w_words, w_scales, wgo, offs, out):
         quantize(3, 1, 64, 128)
         for h in range(HALVES):
             for m in range(M_TILES):
-                multiply(m, h, [3, 0, 1, 2] if h else [0, 1, 3, 2])
+                multiply(m, h, [[[0, 1, 3, 2], [2, 0, 3, 1]], [[0, 1, 3, 2], [3, 0, 1, 2]]][m][h])
                 leave_psum(m, h)
                 scatter(m, h)
                 if h == 1:

@@ -153,43 +153,61 @@ def tile_list_hscat_none_kernel(tc, x, w_words, w_scales, wgo, offs, out):
         def store(m, queue=nc.sync):
             queue.dma_start(out=out[m * P : (m + 1) * P, :], in_=windows[m][:])
 
-        def warm_up():
-            spare = psum.tile([32, HALF], F32, name="spare", tag="bank_spare")
-            for i in range(6):
+        def load_weight_rows(queue):
+            pieces = tile([P, QUADRANT], F32, "weight_pieces")
+            queue.dma_start(out=pieces[:], in_=wgo[0:P:8, :].rearrange("s (b c) -> s b c", c=QUADRANT))
+            return pieces
+
+        def spread_weights(pieces):
+            turned = tile([P, QUADRANT], F32, "weights_turned")
+            nc.vector.transpose(turned[:], pieces[:])
+            repeated = tile([P, S], F32, "weights_repeated")
+            nc.vector.tensor_copy(
+                out=repeated[:].rearrange("p (b s i) -> p b s i", s=4, i=8),
+                in_=turned[:].rearrange("p (s b) -> p b s", b=8).unsqueeze(3).to_broadcast([P, 8, 4, 8]),
+            )
+            spread = tile([P, S], F32, "weights")
+            nc.vector.transpose(spread[:], repeated[:])
+            for h in range(HALVES):
+                weights[h] = spread[:, h * HALF : (h + 1) * HALF]
+
+        spare = psum.tile([32, HALF], F32, name="spare", tag="bank_spare")
+
+        def warm_up(a, h, passes):
+            for _ in range(passes):
                 nc.tensor.matmul_mx(
                     out=spare[:],
-                    lhsT=x_codes[0, 1][:, 0:32].bitcast(FP8X4),
+                    lhsT=x_codes[a, h][:, 0:32].bitcast(FP8X4),
                     lhsT_scale=w_scale_rows[:, 0:32],
-                    rhs=x_codes[0, 1][:].bitcast(FP8X4),
-                    rhs_scale=x_scales[0, 1][:],
+                    rhs=x_codes[a, h][:].bitcast(FP8X4),
+                    rhs_scale=x_scales[a, h][:],
                     start=True,
                     stop=True,
                 )
 
-        load_scales(nc.scalar, [1, 2, 3])
-        load_x_pair(0)
-        load_scales(nc.sync, [0])
+        load_scales()
         load_x(3, 0, 1)
+        pieces = load_weight_rows(nc.sync)
+        load_x(0, 0, 2)
+        load_x(1, 0, 2)
         load_x(2, 0, 2)
         load_w(0, 1, 0, 2)
         load_w(0, 1, 2, 4)
         load_x(3, 1, 2)
         load_w(1, 2, 0, 4)
-        load_weights(0, 1)
         load_lists()
-        load_weights(1, 2)
 
+        round_shared(3, 0)
+        quantize(3, 0)
+        spread_weights(pieces)
         for a in range(2):
             round_cols(a, 0, on_vector, 0, HALF)
             round_cols(a, 1, on_scalar, 0, HALF)
-        for a in range(2):
             quantize(a, 0)
-        round_cols(3, 0, on_scalar, 0, HALF)
-        quantize(0, 1)
-        warm_up()
-        quantize(1, 1)
+            quantize(a, 1)
+        warm_up(0, 1, 3)
+        warm_up(1, 0, 3)
         round_shared(2, 0, 96)
-        quantize(3, 0)
         quantize(2, 0)
         round_cols(2, 1, on_scalar, 0, HALF)
         quantize(2, 1)

@@ -205,8 +205,8 @@ def tile_list_hscat_none_kernel(tc, x, w_words, w_scales, wgo, offs, out):
             round_cols(a, 1, on_scalar, 0, HALF)
             quantize(a, 0)
             quantize(a, 1)
-        warm_up(0, 1, 3)
-        warm_up(1, 0, 3)
+        warm_up(0, 1, 2)
+        warm_up(1, 0, 4)
         round_shared(2, 0, 96)
         quantize(2, 0)
         round_cols(2, 1, on_scalar, 0, HALF)

@@ -207,9 +207,10 @@ def tile_list_hscat_none_kernel(tc, x, w_words, w_scales, wgo, offs, out):
             quantize(a, 1)
         warm_up(0, 1, 2)
         warm_up(1, 0, 4)
-        round_shared(2, 0, 96)
-        quantize(2, 0)
-        round_cols(2, 1, on_scalar, 0, HALF)
+        round_shared(2, 0, 64)
+        round_shared(2, 1, 64)
+        quantize(2, 0, 0, 64)
+        quantize(2, 0, 64, 128)
         quantize(2, 1)
         round_cols(3, 1, on_vector, 0, 64)
         round_cols(3, 1, on_vector, 64, 128)

@@ -190,9 +190,9 @@ def tile_list_hscat_none_kernel(tc, x, w_words, w_scales, wgo, offs, out):
         pieces = load_weight_rows(nc.sync)
         load_x(0, 0, 2)
         load_x(1, 0, 2)
+        load_w(0, 1, 0, 1)
         load_x(2, 0, 2)
-        load_w(0, 1, 0, 2)
-        load_w(0, 1, 2, 4)
+        load_w(0, 1, 1, 4)
         load_x(3, 1, 2)
         load_w(1, 2, 0, 4)
         load_lists()
@@ -205,8 +205,8 @@ def tile_list_hscat_none_kernel(tc, x, w_words, w_scales, wgo, offs, out):
             round_cols(a, 1, on_scalar, 0, HALF)
             quantize(a, 0)
             quantize(a, 1)
-        warm_up(0, 1, 2)
-        warm_up(1, 0, 4)
+        warm_up(0, 1, 3)
+        warm_up(1, 0, 3)
         round_shared(2, 0, 64)
         round_shared(2, 1, 64)
         quantize(2, 0, 0, 64)
@@ -218,7 +218,7 @@ def tile_list_hscat_none_kernel(tc, x, w_words, w_scales, wgo, offs, out):
         quantize(3, 1, 64, 128)
         for h in range(HALVES):
             for m in range(M_TILES):
-                multiply(m, h, [[[0, 1, 3, 2], [2, 0, 3, 1]], [[0, 1, 3, 2], [3, 0, 1, 2]]][m][h])
+                multiply(m, h, [[[0, 1, 3, 2], [0, 2, 1, 3]], [[0, 1, 3, 2], [3, 0, 1, 2]]][m][h])
                 leave_psum(m, h)
                 scatter(m, h)
                 if h == 1:

@@ -190,23 +190,23 @@ def tile_list_hscat_none_kernel(tc, x, w_words, w_scales, wgo, offs, out):
         pieces = load_weight_rows(nc.sync)
         load_x(0, 0, 2)
         load_x(1, 0, 2)
-        load_w(0, 1, 0, 1)
         load_x(2, 0, 2)
-        load_w(0, 1, 1, 4)
+        load_w(0, 1, 0, 4)
         load_x(3, 1, 2)
-        load_w(1, 2, 0, 4)
+        load_w(1, 2, 0, 2)
         load_lists()
 
-        round_shared(3, 0)
+        round_cols(3, 0, on_vector, 0, 64, "first_rounded")
+        round_cols(3, 0, on_scalar, 64, HALF)
         quantize(3, 0)
+        load_w(1, 2, 2, 4, nc.scalar, "first_rounded")
         spread_weights(pieces)
         for a in range(2):
             round_cols(a, 0, on_vector, 0, HALF)
             round_cols(a, 1, on_scalar, 0, HALF)
             quantize(a, 0)
             quantize(a, 1)
-        warm_up(0, 1, 3)
-        warm_up(1, 0, 3)
+        warm_up(1, 0, 6)
         round_shared(2, 0, 64)
         round_shared(2, 1, 64)
         quantize(2, 0, 0, 64)
@@ -218,7 +218,7 @@ def tile_list_hscat_none_kernel(tc, x, w_words, w_scales, wgo, offs, out):
         quantize(3, 1, 64, 128)
         for h in range(HALVES):
             for m in range(M_TILES):
-                multiply(m, h, [[[0, 1, 3, 2], [0, 2, 1, 3]], [[0, 1, 3, 2], [3, 0, 1, 2]]][m][h])
+                multiply(m, h, [[[3, 0, 1, 2], [0, 1, 2, 3]], [[0, 1, 2, 3], [3, 0, 1, 2]]][m][h])
                 leave_psum(m, h)
                 scatter(m, h)
                 if h == 1:

@@ -196,16 +196,19 @@ def tile_list_hscat_none_kernel(tc, x, w_words, w_scales, wgo, offs, out):
         load_w(1, 2, 0, 2)
         load_lists()
 
-        round_cols(3, 0, on_vector, 0, 64, "first_rounded")
+        round_cols(3, 0, on_vector, 0, 64)
         round_cols(3, 0, on_scalar, 64, HALF)
         quantize(3, 0)
-        load_w(1, 2, 2, 4, nc.scalar, "first_rounded")
         spread_weights(pieces)
-        for a in range(2):
-            round_cols(a, 0, on_vector, 0, HALF)
-            round_cols(a, 1, on_scalar, 0, HALF)
-            quantize(a, 0)
-            quantize(a, 1)
+        round_cols(0, 0, on_vector, 0, HALF)
+        round_cols(0, 1, on_scalar, 0, HALF, "handed_on")
+        quantize(0, 0)
+        quantize(0, 1)
+        load_w(1, 2, 2, 4, nc.scalar, "handed_on")
+        round_cols(1, 0, on_vector, 0, HALF)
+        round_cols(1, 1, on_scalar, 0, HALF)
+        quantize(1, 0)
+        quantize(1, 1)
         warm_up(1, 0, 6)
         round_shared(2, 0, 64)
         round_shared(2, 1, 64)

@@ -178,7 +178,7 @@ def tile_list_hscat_none_kernel(tc, x, w_words, w_scales, wgo, offs, out):
                 nc.tensor.matmul_mx(
                     out=spare[:],
                     lhsT=x_codes[a, h][:, 0:32].bitcast(FP8X4),
-                    lhsT_scale=w_scale_rows[:, 0:32],
+                    lhsT_scale=x_scales[a, h][:, 0:32],
                     rhs=x_codes[a, h][:].bitcast(FP8X4),
                     rhs_scale=x_scales[a, h][:],
                     start=True,
@@ -209,7 +209,8 @@ def tile_list_hscat_none_kernel(tc, x, w_words, w_scales, wgo, offs, out):
         round_cols(1, 1, on_scalar, 0, HALF)
         quantize(1, 0)
         quantize(1, 1)
-        warm_up(1, 0, 6)
+        warm_up(0, 1, 3)
+        warm_up(1, 0, 3)
         round_shared(2, 0, 64)
         round_shared(2, 1, 64)
         quantize(2, 0, 0, 64)
@@ -221,7 +222,7 @@ def tile_list_hscat_none_kernel(tc, x, w_words, w_scales, wgo, offs, out):
         quantize(3, 1, 64, 128)
         for h in range(HALVES):
             for m in range(M_TILES):
-                multiply(m, h, [[[3, 0, 1, 2], [0, 1, 2, 3]], [[0, 1, 2, 3], [3, 0, 1, 2]]][m][h])
+                multiply(m, h, [[[3, 0, 1, 2], [3, 0, 1, 2]], [[0, 1, 2, 3], [3, 0, 1, 2]]][m][h])
                 leave_psum(m, h)
                 scatter(m, h)
                 if h == 1:

@@ -173,22 +173,23 @@ def tile_list_hscat_none_kernel(tc, x, w_words, w_scales, wgo, offs, out):
 
         spare = psum.tile([32, HALF], F32, name="spare", tag="bank_spare")
 
-        def warm_up(a, h, passes):
+        def warm_up(a, h, passes, scale_rows=w_scale_rows):
             for _ in range(passes):
                 nc.tensor.matmul_mx(
                     out=spare[:],
                     lhsT=x_codes[a, h][:, 0:32].bitcast(FP8X4),
-                    lhsT_scale=x_scales[a, h][:, 0:32],
+                    lhsT_scale=scale_rows[:, 0:32],
                     rhs=x_codes[a, h][:].bitcast(FP8X4),
                     rhs_scale=x_scales[a, h][:],
                     start=True,
                     stop=True,
                 )
 
-        load_scales()
+        load_scales(nc.scalar, range(3))
         load_x(3, 0, 1)
         pieces = load_weight_rows(nc.sync)
         load_x(0, 0, 2)
+        load_scales(nc.sync, [3])
         load_x(1, 0, 2)
         load_x(2, 0, 2)
         load_w(0, 1, 0, 4)
@@ -209,7 +210,7 @@ def tile_list_hscat_none_kernel(tc, x, w_words, w_scales, wgo, offs, out):
         round_cols(1, 1, on_scalar, 0, HALF)
         quantize(1, 0)
         quantize(1, 1)
-        warm_up(0, 1, 3)
+        warm_up(0, 1, 3, x_scales[0, 1])
         warm_up(1, 0, 3)
         round_shared(2, 0, 64)
         round_shared(2, 1, 64)

@@ -122,9 +122,9 @@ def tile_list_hscat_none_kernel(tc, x, w_words, w_scales, wgo, offs, out):
                 in_=rounded[a, h][:, c0:c1, :].rearrange("p j t -> p (j t)"),
             )
 
-        def multiply(m, h, passes):
+        def multiply(m, h, passes, bank=None):
             if (m, h) not in totals:
-                totals[m, h] = psum.tile([P, HALF], F32, name=f"total_{m}_{h}", tag=f"bank_{m}_{h}")
+                totals[m, h] = psum.tile([P, HALF], F32, name=f"total_{m}_{h}", tag=bank or f"bank_{m}_{h}")
                 passes_done[m, h] = []
             for a in passes:
                 passes_done[m, h].append(a)
@@ -173,11 +173,11 @@ def tile_list_hscat_none_kernel(tc, x, w_words, w_scales, wgo, offs, out):
 
         spare = psum.tile([32, HALF], F32, name="spare", tag="bank_spare")
 
-        def warm_up(a, h, passes, scale_rows=w_scale_rows):
+        def warm_up(a, h, passes, scale_rows=w_scale_rows, stationary=None):
             for _ in range(passes):
                 nc.tensor.matmul_mx(
                     out=spare[:],
-                    lhsT=x_codes[a, h][:, 0:32].bitcast(FP8X4),
+                    lhsT=(x_codes[a, h] if stationary is None else stationary)[:, 0:32].bitcast(FP8X4),
                     lhsT_scale=scale_rows[:, 0:32],
                     rhs=x_codes[a, h][:].bitcast(FP8X4),
                     rhs_scale=x_scales[a, h][:],
@@ -185,33 +185,27 @@ def tile_list_hscat_none_kernel(tc, x, w_words, w_scales, wgo, offs, out):
                     stop=True,
                 )
 
-        load_scales(nc.scalar, range(3))
+        load_scales()
         load_x(3, 0, 1)
         pieces = load_weight_rows(nc.sync)
         load_x(0, 0, 2)
-        load_scales(nc.sync, [3])
         load_x(1, 0, 2)
         load_x(2, 0, 2)
         load_w(0, 1, 0, 4)
         load_x(3, 1, 2)
         load_w(1, 2, 0, 2)
+        load_w(1, 2, 2, 4)
         load_lists()
 
-        round_cols(3, 0, on_vector, 0, 64)
-        round_cols(3, 0, on_scalar, 64, HALF)
+        round_shared(3, 0)
         quantize(3, 0)
         spread_weights(pieces)
-        round_cols(0, 0, on_vector, 0, HALF)
-        round_cols(0, 1, on_scalar, 0, HALF, "handed_on")
-        quantize(0, 0)
-        quantize(0, 1)
-        load_w(1, 2, 2, 4, nc.scalar, "handed_on")
-        round_cols(1, 0, on_vector, 0, HALF)
-        round_cols(1, 1, on_scalar, 0, HALF)
-        quantize(1, 0)
-        quantize(1, 1)
-        warm_up(0, 1, 3, x_scales[0, 1])
-        warm_up(1, 0, 3)
+        for a in range(2):
+            round_cols(a, 0, on_vector, 0, HALF)
+            round_cols(a, 1, on_scalar, 0, HALF)
+            quantize(a, 0)
+            quantize(a, 1)
+        warm_up(1, 0, 5)
         round_shared(2, 0, 64)
         round_shared(2, 1, 64)
         quantize(2, 0, 0, 64)
@@ -221,10 +215,18 @@ def tile_list_hscat_none_kernel(tc, x, w_words, w_scales, wgo, offs, out):
         round_cols(3, 1, on_vector, 64, 128)
         quantize(3, 1, 0, 64)
         quantize(3, 1, 64, 128)
-        for h in range(HALVES):
-            for m in range(M_TILES):
-                multiply(m, h, [[[3, 0, 1, 2], [3, 0, 1, 2]], [[0, 1, 2, 3], [3, 0, 1, 2]]][m][h])
-                leave_psum(m, h)
-                scatter(m, h)
-                if h == 1:
-                    store(m)
+        multiply(0, 0, [3, 0, 1, 2])
+        leave_psum(0, 0)
+        scatter(0, 0)
+        multiply(1, 0, [0, 1, 2, 3])
+        warm_up(0, 0, 1, w_scale_rows, w_codes[1, 3])
+        leave_psum(1, 0)
+        scatter(1, 0)
+        multiply(0, 1, [0, 1, 2, 3], "bank_spare")
+        leave_psum(0, 1)
+        scatter(0, 1)
+        store(0)
+        multiply(1, 1, [3, 2, 1, 0])
+        leave_psum(1, 1)
+        scatter(1, 1)
+        store(1)

@@ -200,11 +200,14 @@ def tile_list_hscat_none_kernel(tc, x, w_words, w_scales, wgo, offs, out):
         round_shared(3, 0)
         quantize(3, 0)
         spread_weights(pieces)
-        for a in range(2):
-            round_cols(a, 0, on_vector, 0, HALF)
-            round_cols(a, 1, on_scalar, 0, HALF)
-            quantize(a, 0)
-            quantize(a, 1)
+        round_cols(0, 0, on_vector, 0, HALF)
+        round_cols(0, 1, on_scalar, 0, HALF)
+        quantize(0, 0)
+        quantize(0, 1)
+        round_shared(1, 0, 64)
+        round_shared(1, 1, 64)
+        quantize(1, 0)
+        quantize(1, 1)
         warm_up(1, 0, 5)
         round_shared(2, 0, 64)
         round_shared(2, 1, 64)

@@ -124,7 +124,7 @@ def tile_list_hscat_none_kernel(tc, x, w_words, w_scales, wgo, offs, out):
 
         def multiply(m, h, passes, bank=None):
             if (m, h) not in totals:
-                totals[m, h] = psum.tile([P, HALF], F32, name=f"total_{m}_{h}", tag=bank or f"bank_{m}_{h}")
+                totals[m, h] = psum.tile([P, HALF], F32, name=f"total_{m}_{h}", tag=f"bank_{m}_{h}") if bank is None else bank
                 passes_done[m, h] = []
             for a in passes:
                 passes_done[m, h].append(a)
@@ -171,7 +171,8 @@ def tile_list_hscat_none_kernel(tc, x, w_words, w_scales, wgo, offs, out):
             for h in range(HALVES):
                 weights[h] = spread[:, h * HALF : (h + 1) * HALF]
 
-        spare = psum.tile([32, HALF], F32, name="spare", tag="bank_spare")
+        shared = psum.tile([P, S], F32, name="shared", tag="bank_shared")
+        spare = shared[0:32, HALF:]
 
         def warm_up(a, h, passes, scale_rows=w_scale_rows, stationary=None):
             for _ in range(passes):
@@ -225,7 +226,7 @@ def tile_list_hscat_none_kernel(tc, x, w_words, w_scales, wgo, offs, out):
         warm_up(0, 0, 1, w_scale_rows, w_codes[1, 3])
         leave_psum(1, 0)
         scatter(1, 0)
-        multiply(0, 1, [0, 1, 2, 3], "bank_spare")
+        multiply(0, 1, [0, 1, 2, 3], shared[:, :HALF])
         leave_psum(0, 1)
         scatter(0, 1)
         store(0)

@@ -172,7 +172,7 @@ def tile_list_hscat_none_kernel(tc, x, w_words, w_scales, wgo, offs, out):
                 weights[h] = spread[:, h * HALF : (h + 1) * HALF]
 
         shared = psum.tile([P, S], F32, name="shared", tag="bank_shared")
-        spare = shared[0:32, HALF:]
+        spare = psum.tile([32, HALF], F32, name="spare", tag="bank_spare")
 
         def warm_up(a, h, passes, scale_rows=w_scale_rows, stationary=None):
             for _ in range(passes):
@@ -209,7 +209,8 @@ def tile_list_hscat_none_kernel(tc, x, w_words, w_scales, wgo, offs, out):
         round_shared(1, 1, 64)
         quantize(1, 0)
         quantize(1, 1)
-        warm_up(1, 0, 5)
+        warm_up(1, 0, 5, x_scales[1, 0])
+        warm_up(1, 0, 1)
         round_shared(2, 0, 64)
         round_shared(2, 1, 64)
         quantize(2, 0, 0, 64)
@@ -223,14 +224,13 @@ def tile_list_hscat_none_kernel(tc, x, w_words, w_scales, wgo, offs, out):
         leave_psum(0, 0)
         scatter(0, 0)
         multiply(1, 0, [0, 1, 2, 3])
-        warm_up(0, 0, 1, w_scale_rows, w_codes[1, 3])
         leave_psum(1, 0)
         scatter(1, 0)
+        multiply(1, 1, [2, 0, 1, 3], shared[:, HALF:])
         multiply(0, 1, [0, 1, 2, 3], shared[:, :HALF])
         leave_psum(0, 1)
         scatter(0, 1)
         store(0)
-        multiply(1, 1, [3, 2, 1, 0])
         leave_psum(1, 1)
         scatter(1, 1)
         store(1)

@@ -207,9 +207,10 @@ def tile_list_hscat_none_kernel(tc, x, w_words, w_scales, wgo, offs, out):
         quantize(0, 1)
         round_shared(1, 0, 64)
         round_shared(1, 1, 64)
-        quantize(1, 0)
+        quantize(1, 0, 0, 64)
+        quantize(1, 0, 64, 128)
         quantize(1, 1)
-        warm_up(1, 0, 5, x_scales[1, 0])
+        warm_up(0, 0, 5, x_scales[1, 0], x_codes[1, 0])
         warm_up(1, 0, 1)
         round_shared(2, 0, 64)
         round_shared(2, 1, 64)

@@ -212,10 +212,9 @@ def tile_list_hscat_none_kernel(tc, x, w_words, w_scales, wgo, offs, out):
         quantize(1, 1)
         warm_up(0, 0, 5, x_scales[1, 0], x_codes[1, 0])
         warm_up(1, 0, 1)
-        round_shared(2, 0, 64)
-        round_shared(2, 1, 64)
-        quantize(2, 0, 0, 64)
-        quantize(2, 0, 64, 128)
+        round_cols(2, 0, on_vector, 0, HALF)
+        round_cols(2, 1, on_scalar, 0, HALF)
+        quantize(2, 0)
         quantize(2, 1)
         round_cols(3, 1, on_vector, 0, 64)
         round_cols(3, 1, on_vector, 64, 128)

@@ -198,15 +198,16 @@ def tile_list_hscat_none_kernel(tc, x, w_words, w_scales, wgo, offs, out):
         load_w(1, 2, 2, 4)
         load_lists()
 
-        round_shared(3, 0)
+        round_cols(3, 0, on_scalar, 0, HALF)
         quantize(3, 0)
         spread_weights(pieces)
         round_cols(0, 0, on_vector, 0, HALF)
         round_cols(0, 1, on_scalar, 0, HALF)
         quantize(0, 0)
         quantize(0, 1)
-        round_shared(1, 0, 64)
-        round_shared(1, 1, 64)
+        round_cols(1, 0, on_vector, 0, 64)
+        round_cols(1, 0, on_vector, 64, HALF)
+        round_cols(1, 1, on_scalar, 0, HALF)
         quantize(1, 0, 0, 64)
         quantize(1, 0, 64, 128)
         quantize(1, 1)

@@ -18,8 +18,10 @@ P = 128
 PACK = 4
 K_PASS = P * PACK
 PASSES = K // K_PASS
+LAST = PASSES - 1
+MID = PASSES // 2
 HALF = S // 2
-HALVES = S // HALF
+PART = HALF // 2
 M_TILES = M // P
 QUADRANT = 32
 SCALE_ROWS = 4
@@ -27,6 +29,8 @@ GROUP = 16
 LIST_COLS = HALF // GROUP
 LINE = 4
 ALIGN = 256
+WARM_M = 32
+WARM_PASSES = 6
 
 
 def tile_list_hscat_none_kernel(tc, x, w_words, w_scales, wgo, offs, out):
@@ -35,82 +39,44 @@ def tile_list_hscat_none_kernel(tc, x, w_words, w_scales, wgo, offs, out):
         keep = ctx.enter_context(tc.tile_pool(name="keep", bufs=1))
         psum = ctx.enter_context(tc.psum_pool(name="psum", bufs=1))
 
-        def tile(shape, dtype, name, tag=None):
-            return keep.tile(shape, dtype, name=name, tag=tag or name, align_bytes=ALIGN)
+        def tile(shape, dtype, name):
+            return keep.tile(shape, dtype, name=name, align_bytes=ALIGN)
 
         w_scale_rows = tile([P, M], U8, "w_scale_rows")
         windows = [tile([P, T], F32, f"window_{m}") for m in range(M_TILES)]
-        for m in range(M_TILES):
-            nc.vector.memset(windows[m][:], 0.0)
+        for window in windows:
+            nc.vector.memset(window[:], 0.0)
 
         offsets = tile([P, S // GROUP], U16, "offsets")
-        x_rows = {}
-        w_codes = {}
-        weights = {}
-        rounded = {}
-        x_codes = {}
-        x_scales = {}
-        totals = {}
-        passes_done = {}
-        results = {}
+        x_rows, rounded, x_codes, x_scales, w_codes = {}, {}, {}, {}, {}
         on_vector = nc.vector.tensor_copy
         on_scalar = nc.scalar.copy
 
-        def load_scales(queue=nc.scalar, quadrants=range(P // QUADRANT)):
-            for q in quadrants:
-                queue.dma_start(
-                    out=w_scale_rows[QUADRANT * q : QUADRANT * q + PASSES * SCALE_ROWS, :].bitcast(I32),
-                    in_=w_scales[:, SCALE_ROWS * q : SCALE_ROWS * (q + 1), :].bitcast(I32),
-                )
-
-        def load_x(a, h0, h1, queue=nc.sync):
+        def load_x(a, h0, h1):
             loaded = tile([P, PACK, (h1 - h0) * HALF], F32, f"x_rows_{a}_{h0}")
             rows = x[a * K_PASS : (a + 1) * K_PASS, h0 * HALF : h1 * HALF]
-            queue.dma_start(out=loaded[:], in_=rows.rearrange("(p t) j -> p t j", t=PACK))
+            nc.sync.dma_start(out=loaded[:], in_=rows.rearrange("(p t) j -> p t j", t=PACK))
             for h in range(h0, h1):
                 x_rows[a, h] = loaded[:, :, (h - h0) * HALF : (h - h0 + 1) * HALF]
 
-        def load_x_pair(a):
-            loaded = tile([P, 2, PACK, S], F32, f"x_rows_{a}_0")
-            rows = x[a * K_PASS : (a + 2) * K_PASS, :]
-            nc.sync.dma_start(
-                out=loaded[:].rearrange("p b t j -> p b (t j)"),
-                in_=rows.rearrange("(b p t) j -> p b (t j)", b=2, t=PACK),
-            )
-            for b in range(2):
-                for h in range(HALVES):
-                    x_rows[a + b, h] = loaded[:, b, :, h * HALF : (h + 1) * HALF]
+        def load_w(m, a0, a1):
+            loaded = tile([P, a1 - a0, P], U32, f"w_codes_{m}_{a0}")
+            words = w_words[a0:a1, :, m * P : (m + 1) * P, :].rearrange("a p n t -> p a (n t)")
+            nc.sync.dma_start(out=loaded[:].bitcast(I32), in_=words.bitcast(I32))
+            for a in range(a0, a1):
+                w_codes[m, a] = loaded[:, a - a0, :]
 
-        def load_w(m0, m1, a0, a1, queue=nc.sync, tag=None):
-            loaded = tile([P, a1 - a0, (m1 - m0) * P], U32, f"w_codes_{m0}_{a0}", tag)
-            queue.dma_start(
-                out=loaded[:].bitcast(I32),
-                in_=w_words[a0:a1, :, m0 * P : m1 * P, :].rearrange("a p n t -> p a (n t)").bitcast(I32),
-            )
-            for m in range(m0, m1):
-                for a in range(a0, a1):
-                    w_codes[m, a] = loaded[:, a - a0, (m - m0) * P : (m - m0 + 1) * P]
-
-        def load_weights(h0, h1, queue=nc.sync):
-            loaded = tile([P, (h1 - h0) * HALF], F32, f"weights_{h0}")
-            queue.dma_start(out=loaded[:], in_=wgo[:, h0 * HALF : h1 * HALF])
-            for h in range(h0, h1):
-                weights[h] = loaded[:, (h - h0) * HALF : (h - h0 + 1) * HALF]
-
-        def load_lists():
-            nc.sync.dma_start(offsets[:], offs)
-
-        def round_cols(a, h, copy, c0, c1, tag=None):
+        def round_cols(a, h, copy, c0=0, c1=HALF):
             if (a, h) not in rounded:
-                rounded[a, h] = tile([P, HALF, PACK], BF16, f"rounded_{a}_{h}", tag)
+                rounded[a, h] = tile([P, HALF, PACK], BF16, f"rounded_{a}_{h}")
             copy(
                 out=rounded[a, h][:, c0:c1, :].rearrange("p (c i) t -> p c t i", i=LINE),
                 in_=x_rows[a, h][:, :, c0:c1].rearrange("p t (c i) -> p c t i", i=LINE),
             )
 
-        def round_shared(a, h, on_v=HALF // 2):
-            round_cols(a, h, on_vector, 0, on_v)
-            round_cols(a, h, on_scalar, on_v, HALF)
+        def round_in_parts(a, h):
+            round_cols(a, h, on_vector, 0, PART)
+            round_cols(a, h, on_vector, PART, HALF)
 
         def quantize(a, h, c0=0, c1=HALF):
             if (a, h) not in x_codes:
@@ -122,116 +88,107 @@ def tile_list_hscat_none_kernel(tc, x, w_words, w_scales, wgo, offs, out):
                 in_=rounded[a, h][:, c0:c1, :].rearrange("p j t -> p (j t)"),
             )
 
-        def multiply(m, h, passes, bank=None):
-            if (m, h) not in totals:
-                totals[m, h] = psum.tile([P, HALF], F32, name=f"total_{m}_{h}", tag=f"bank_{m}_{h}") if bank is None else bank
-                passes_done[m, h] = []
+        def quantize_in_parts(a, h):
+            quantize(a, h, 0, PART)
+            quantize(a, h, PART, HALF)
+
+        warm_bank = psum.tile([WARM_M, HALF], F32, name="warm_bank")
+
+        def warm_up(scale_rows, a):
+            nc.tensor.matmul_mx(
+                out=warm_bank[:],
+                lhsT=x_codes[1, 0][:, :WARM_M].bitcast(FP8X4),
+                lhsT_scale=scale_rows[:, :WARM_M],
+                rhs=x_codes[a, 0][:].bitcast(FP8X4),
+                rhs_scale=x_scales[a, 0][:],
+                start=True,
+                stop=True,
+            )
+
+        def multiply(m, h, total, passes):
             for a in passes:
-                passes_done[m, h].append(a)
                 nc.tensor.matmul_mx(
-                    out=totals[m, h][:],
+                    out=total,
                     lhsT=w_codes[m, a].bitcast(FP8X4),
                     lhsT_scale=w_scale_rows[SCALE_ROWS * a :, m * P : (m + 1) * P],
                     rhs=x_codes[a, h][:].bitcast(FP8X4),
                     rhs_scale=x_scales[a, h][:],
-                    start=len(passes_done[m, h]) == 1,
-                    stop=len(passes_done[m, h]) == PASSES,
+                    start=a == passes[0],
+                    stop=a == passes[-1],
                 )
 
-        def leave_psum(m, h, copy=on_scalar, tag=None):
-            results[m, h] = tile([P, HALF], F32, f"y_{m}_{h}", tag)
-            copy(out=results[m, h][:], in_=totals[m, h][:])
-
-        def scatter(m, h):
+        def place(m, h, total):
+            result = tile([P, HALF], F32, f"y_{m}_{h}")
+            on_scalar(out=result[:], in_=total)
             nc.vector.tensor_tensor(
                 windows[m][:].indirect(offsets[:, LIST_COLS * h : LIST_COLS * (h + 1)]),
-                results[m, h][:],
-                weights[h],
+                result[:],
+                weights[:, h * HALF : (h + 1) * HALF],
                 MULT,
             )
 
-        def store(m, queue=nc.sync):
-            queue.dma_start(out=out[m * P : (m + 1) * P, :], in_=windows[m][:])
+        def store(m):
+            nc.sync.dma_start(out=out[m * P : (m + 1) * P, :], in_=windows[m][:])
 
-        def load_weight_rows(queue):
-            pieces = tile([P, QUADRANT], F32, "weight_pieces")
-            queue.dma_start(out=pieces[:], in_=wgo[0:P:8, :].rearrange("s (b c) -> s b c", c=QUADRANT))
-            return pieces
-
-        def spread_weights(pieces):
-            turned = tile([P, QUADRANT], F32, "weights_turned")
-            nc.vector.transpose(turned[:], pieces[:])
-            repeated = tile([P, S], F32, "weights_repeated")
-            nc.vector.tensor_copy(
-                out=repeated[:].rearrange("p (b s i) -> p b s i", s=4, i=8),
-                in_=turned[:].rearrange("p (s b) -> p b s", b=8).unsqueeze(3).to_broadcast([P, 8, 4, 8]),
+        for quadrant in range(P // QUADRANT):
+            first = QUADRANT * quadrant
+            nc.scalar.dma_start(
+                out=w_scale_rows[first : first + PASSES * SCALE_ROWS, :].bitcast(I32),
+                in_=w_scales[:, SCALE_ROWS * quadrant : SCALE_ROWS * (quadrant + 1), :].bitcast(I32),
             )
-            spread = tile([P, S], F32, "weights")
-            nc.vector.transpose(spread[:], repeated[:])
-            for h in range(HALVES):
-                weights[h] = spread[:, h * HALF : (h + 1) * HALF]
 
-        shared = psum.tile([P, S], F32, name="shared", tag="bank_shared")
-        spare = psum.tile([32, HALF], F32, name="spare", tag="bank_spare")
+        load_x(LAST, 0, 1)
+        pieces = tile([P, QUADRANT], F32, "weight_pieces")
+        nc.sync.dma_start(out=pieces[:], in_=wgo[0:P:8, :].rearrange("s (b c) -> s b c", c=QUADRANT))
+        for a in range(LAST):
+            load_x(a, 0, 2)
+        load_w(0, 0, PASSES)
+        load_x(LAST, 1, 2)
+        load_w(1, MID, PASSES)
+        load_w(1, 0, MID)
+        nc.sync.dma_start(offsets[:], offs)
 
-        def warm_up(a, h, passes, scale_rows=w_scale_rows, stationary=None):
-            for _ in range(passes):
-                nc.tensor.matmul_mx(
-                    out=spare[:],
-                    lhsT=(x_codes[a, h] if stationary is None else stationary)[:, 0:32].bitcast(FP8X4),
-                    lhsT_scale=scale_rows[:, 0:32],
-                    rhs=x_codes[a, h][:].bitcast(FP8X4),
-                    rhs_scale=x_scales[a, h][:],
-                    start=True,
-                    stop=True,
-                )
+        round_cols(LAST, 0, on_scalar)
+        quantize(LAST, 0)
 
-        load_scales()
-        load_x(3, 0, 1)
-        pieces = load_weight_rows(nc.sync)
-        load_x(0, 0, 2)
-        load_x(1, 0, 2)
-        load_x(2, 0, 2)
-        load_w(0, 1, 0, 4)
-        load_x(3, 1, 2)
-        load_w(1, 2, 0, 2)
-        load_w(1, 2, 2, 4)
-        load_lists()
+        turned = tile([P, QUADRANT], F32, "weights_turned")
+        nc.vector.transpose(turned[:], pieces[:])
+        repeated = tile([P, S], F32, "weights_repeated")
+        nc.vector.tensor_copy(
+            out=repeated[:].rearrange("p (b s i) -> p b s i", s=4, i=8),
+            in_=turned[:].rearrange("p (s b) -> p b s", b=8).unsqueeze(3).to_broadcast([P, 8, 4, 8]),
+        )
+        weights = tile([P, S], F32, "weights")
+        nc.vector.transpose(weights[:], repeated[:])
 
-        round_cols(3, 0, on_scalar, 0, HALF)
-        quantize(3, 0)
-        spread_weights(pieces)
-        round_cols(0, 0, on_vector, 0, HALF)
-        round_cols(0, 1, on_scalar, 0, HALF)
+        round_cols(0, 0, on_vector)
+        round_cols(0, 1, on_scalar)
         quantize(0, 0)
         quantize(0, 1)
-        round_cols(1, 0, on_vector, 0, 64)
-        round_cols(1, 0, on_vector, 64, HALF)
-        round_cols(1, 1, on_scalar, 0, HALF)
-        quantize(1, 0, 0, 64)
-        quantize(1, 0, 64, 128)
+        round_in_parts(1, 0)
+        round_cols(1, 1, on_scalar)
+        quantize_in_parts(1, 0)
         quantize(1, 1)
-        warm_up(0, 0, 5, x_scales[1, 0], x_codes[1, 0])
-        warm_up(1, 0, 1)
-        round_cols(2, 0, on_vector, 0, HALF)
-        round_cols(2, 1, on_scalar, 0, HALF)
+        for _ in range(WARM_PASSES - 1):
+            warm_up(x_scales[1, 0], 0)
+        warm_up(w_scale_rows, 1)
+        round_cols(2, 0, on_vector)
+        round_cols(2, 1, on_scalar)
         quantize(2, 0)
         quantize(2, 1)
-        round_cols(3, 1, on_vector, 0, 64)
-        round_cols(3, 1, on_vector, 64, 128)
-        quantize(3, 1, 0, 64)
-        quantize(3, 1, 64, 128)
-        multiply(0, 0, [3, 0, 1, 2])
-        leave_psum(0, 0)
-        scatter(0, 0)
-        multiply(1, 0, [0, 1, 2, 3])
-        leave_psum(1, 0)
-        scatter(1, 0)
-        multiply(1, 1, [2, 0, 1, 3], shared[:, HALF:])
-        multiply(0, 1, [0, 1, 2, 3], shared[:, :HALF])
-        leave_psum(0, 1)
-        scatter(0, 1)
-        store(0)
-        leave_psum(1, 1)
-        scatter(1, 1)
-        store(1)
+        round_in_parts(LAST, 1)
+        quantize_in_parts(LAST, 1)
+
+        in_turn = list(range(PASSES))
+        first_sum = psum.tile([P, HALF], F32, name="first_sum")
+        multiply(0, 0, first_sum[:], [LAST] + in_turn[:LAST])
+        place(0, 0, first_sum[:])
+        second_sum = psum.tile([P, HALF], F32, name="second_sum")
+        multiply(1, 0, second_sum[:], in_turn[MID:] + in_turn[:MID])
+        place(1, 0, second_sum[:])
+        late_sums = psum.tile([P, S], F32, name="late_sums")
+        multiply(1, 1, late_sums[:, HALF:], in_turn)
+        multiply(0, 1, late_sums[:, :HALF], in_turn)
+        for m, total in enumerate((late_sums[:, :HALF], late_sums[:, HALF:])):
+            place(m, 1, total)
+            store(m)

@@ -19,7 +19,6 @@ PACK = 4
 K_PASS = P * PACK
 PASSES = K // K_PASS
 LAST = PASSES - 1
-MID = PASSES // 2
 HALF = S // 2
 PART = HALF // 2
 M_TILES = M // P
@@ -30,7 +29,7 @@ LIST_COLS = HALF // GROUP
 LINE = 4
 ALIGN = 256
 WARM_M = 32
-WARM_PASSES = 6
+EARLY = ((LAST, 0), (0, 0), (0, 1), (1, 0))
 
 
 def tile_list_hscat_none_kernel(tc, x, w_words, w_scales, wgo, offs, out):
@@ -42,7 +41,6 @@ def tile_list_hscat_none_kernel(tc, x, w_words, w_scales, wgo, offs, out):
         def tile(shape, dtype, name):
             return keep.tile(shape, dtype, name=name, align_bytes=ALIGN)
 
-        w_scale_rows = tile([P, M], U8, "w_scale_rows")
         windows = [tile([P, T], F32, f"window_{m}") for m in range(M_TILES)]
         for window in windows:
             nc.vector.memset(window[:], 0.0)
@@ -52,12 +50,19 @@ def tile_list_hscat_none_kernel(tc, x, w_words, w_scales, wgo, offs, out):
         on_vector = nc.vector.tensor_copy
         on_scalar = nc.scalar.copy
 
-        def load_x(a, h0, h1):
-            loaded = tile([P, PACK, (h1 - h0) * HALF], F32, f"x_rows_{a}_{h0}")
-            rows = x[a * K_PASS : (a + 1) * K_PASS, h0 * HALF : h1 * HALF]
-            nc.sync.dma_start(out=loaded[:], in_=rows.rearrange("(p t) j -> p t j", t=PACK))
-            for h in range(h0, h1):
-                x_rows[a, h] = loaded[:, :, (h - h0) * HALF : (h - h0 + 1) * HALF]
+        def load_x(a0, a1, h0, h1):
+            loaded = tile([P, a1 - a0, PACK, (h1 - h0) * HALF], F32, f"x_rows_{a0}_{h0}")
+            rows = x[a0 * K_PASS : a1 * K_PASS, h0 * HALF : h1 * HALF]
+            if h1 - h0 == 2:
+                nc.sync.dma_start(
+                    out=loaded[:].rearrange("p a t j -> p a (t j)"),
+                    in_=rows.rearrange("(a p t) j -> p a (t j)", p=P, t=PACK),
+                )
+            else:
+                nc.sync.dma_start(out=loaded[:, 0], in_=rows.rearrange("(p t) j -> p t j", t=PACK))
+            for a in range(a0, a1):
+                for h in range(h0, h1):
+                    x_rows[a, h] = loaded[:, a - a0, :, (h - h0) * HALF : (h - h0 + 1) * HALF]
 
         def load_w(m, a0, a1):
             loaded = tile([P, a1 - a0, P], U32, f"w_codes_{m}_{a0}")
@@ -78,10 +83,16 @@ def tile_list_hscat_none_kernel(tc, x, w_words, w_scales, wgo, offs, out):
             round_cols(a, h, on_vector, 0, PART)
             round_cols(a, h, on_vector, PART, HALF)
 
+        early_codes = tile([P, len(EARLY) * HALF], U32, "early_codes")
+        early_scales = tile([P, len(EARLY) * HALF], U8, "early_scales")
+        for i, key in enumerate(EARLY):
+            x_codes[key] = early_codes[:, i * HALF : (i + 1) * HALF]
+            x_scales[key] = early_scales[:, i * HALF : (i + 1) * HALF]
+
         def quantize(a, h, c0=0, c1=HALF):
             if (a, h) not in x_codes:
-                x_codes[a, h] = tile([P, HALF], U32, f"x_codes_{a}_{h}")
-                x_scales[a, h] = tile([P, HALF], U8, f"x_scales_{a}_{h}")
+                x_codes[a, h] = tile([P, HALF], U32, f"x_codes_{a}_{h}")[:]
+                x_scales[a, h] = tile([P, HALF], U8, f"x_scales_{a}_{h}")[:]
             nc.vector.quantize_mx(
                 out=x_codes[a, h][:, c0:c1].bitcast(FP8X4),
                 scales=x_scales[a, h][:, c0:c1],
@@ -92,30 +103,20 @@ def tile_list_hscat_none_kernel(tc, x, w_words, w_scales, wgo, offs, out):
             quantize(a, h, 0, PART)
             quantize(a, h, PART, HALF)
 
-        warm_bank = psum.tile([WARM_M, HALF], F32, name="warm_bank")
-
-        def warm_up(scale_rows, a):
+        def product(m, h, a, total, start=False, stop=False):
             nc.tensor.matmul_mx(
-                out=warm_bank[:],
-                lhsT=x_codes[1, 0][:, :WARM_M].bitcast(FP8X4),
-                lhsT_scale=scale_rows[:, :WARM_M],
-                rhs=x_codes[a, 0][:].bitcast(FP8X4),
-                rhs_scale=x_scales[a, 0][:],
-                start=True,
-                stop=True,
+                out=total,
+                lhsT=w_codes[m, a].bitcast(FP8X4),
+                lhsT_scale=w_scale_rows[SCALE_ROWS * a :, m * P : (m + 1) * P],
+                rhs=x_codes[a, h].bitcast(FP8X4),
+                rhs_scale=x_scales[a, h],
+                start=start,
+                stop=stop,
             )
 
-        def multiply(m, h, total, passes):
-            for a in passes:
-                nc.tensor.matmul_mx(
-                    out=total,
-                    lhsT=w_codes[m, a].bitcast(FP8X4),
-                    lhsT_scale=w_scale_rows[SCALE_ROWS * a :, m * P : (m + 1) * P],
-                    rhs=x_codes[a, h][:].bitcast(FP8X4),
-                    rhs_scale=x_scales[a, h][:],
-                    start=a == passes[0],
-                    stop=a == passes[-1],
-                )
+        def group(steps):
+            for i, (m, h, a, total) in enumerate(steps):
+                product(m, h, a, total, start=i == 0, stop=i == len(steps) - 1)
 
         def place(m, h, total):
             result = tile([P, HALF], F32, f"y_{m}_{h}")
@@ -130,22 +131,23 @@ def tile_list_hscat_none_kernel(tc, x, w_words, w_scales, wgo, offs, out):
         def store(m):
             nc.sync.dma_start(out=out[m * P : (m + 1) * P, :], in_=windows[m][:])
 
+        w_scale_rows = tile([P, M], U8, "w_scale_rows")
         for quadrant in range(P // QUADRANT):
-            first = QUADRANT * quadrant
+            rows = slice(QUADRANT * quadrant, QUADRANT * quadrant + PASSES * SCALE_ROWS)
             nc.scalar.dma_start(
-                out=w_scale_rows[first : first + PASSES * SCALE_ROWS, :].bitcast(I32),
+                out=w_scale_rows[rows, :].bitcast(I32),
                 in_=w_scales[:, SCALE_ROWS * quadrant : SCALE_ROWS * (quadrant + 1), :].bitcast(I32),
             )
 
-        load_x(LAST, 0, 1)
+        load_x(LAST, PASSES, 0, 1)
         pieces = tile([P, QUADRANT], F32, "weight_pieces")
         nc.sync.dma_start(out=pieces[:], in_=wgo[0:P:8, :].rearrange("s (b c) -> s b c", c=QUADRANT))
         for a in range(LAST):
-            load_x(a, 0, 2)
+            load_x(a, a + 1, 0, 2)
         load_w(0, 0, PASSES)
-        load_x(LAST, 1, 2)
-        load_w(1, MID, PASSES)
-        load_w(1, 0, MID)
+        load_x(LAST, PASSES, 1, 2)
+        load_w(1, 2, 4)
+        load_w(1, 0, 2)
         nc.sync.dma_start(offsets[:], offs)
 
         round_cols(LAST, 0, on_scalar)
@@ -161,34 +163,37 @@ def tile_list_hscat_none_kernel(tc, x, w_words, w_scales, wgo, offs, out):
         weights = tile([P, S], F32, "weights")
         nc.vector.transpose(weights[:], repeated[:])
 
-        round_cols(0, 0, on_vector)
-        round_cols(0, 1, on_scalar)
-        quantize(0, 0)
-        quantize(0, 1)
-        round_in_parts(1, 0)
-        round_cols(1, 1, on_scalar)
-        quantize_in_parts(1, 0)
-        quantize(1, 1)
-        for _ in range(WARM_PASSES - 1):
-            warm_up(x_scales[1, 0], 0)
-        warm_up(w_scale_rows, 1)
-        round_cols(2, 0, on_vector)
-        round_cols(2, 1, on_scalar)
-        quantize(2, 0)
-        quantize(2, 1)
+        for a in range(LAST):
+            round_cols(a, 0, on_vector)
+            round_cols(a, 1, on_scalar)
+            quantize(a, 0)
+            quantize(a, 1)
         round_in_parts(LAST, 1)
         quantize_in_parts(LAST, 1)
 
-        in_turn = list(range(PASSES))
+        warm_bank = psum.tile([WARM_M, len(EARLY) * HALF], F32, name="warm_bank")
+        nc.tensor.matmul_mx(
+            out=warm_bank[:],
+            lhsT=early_codes[:, :WARM_M].bitcast(FP8X4),
+            lhsT_scale=w_scale_rows[:, :WARM_M],
+            rhs=early_codes[:].bitcast(FP8X4),
+            rhs_scale=early_scales[:],
+            start=True,
+            stop=True,
+        )
+
         first_sum = psum.tile([P, HALF], F32, name="first_sum")
-        multiply(0, 0, first_sum[:], [LAST] + in_turn[:LAST])
+        group([(0, 0, a, first_sum[:]) for a in (LAST, 0, 1, 2)])
         place(0, 0, first_sum[:])
         second_sum = psum.tile([P, HALF], F32, name="second_sum")
-        multiply(1, 0, second_sum[:], in_turn[MID:] + in_turn[:MID])
+        group([(1, 0, a, second_sum[:]) for a in (2, 3, 0, 1)])
         place(1, 0, second_sum[:])
         late_sums = psum.tile([P, S], F32, name="late_sums")
-        multiply(1, 1, late_sums[:, HALF:], in_turn)
-        multiply(0, 1, late_sums[:, :HALF], in_turn)
-        for m, total in enumerate((late_sums[:, :HALF], late_sums[:, HALF:])):
-            place(m, 1, total)
+        late = [late_sums[:, :HALF], late_sums[:, HALF:]]
+        group(
+            [(m, 1, a, late[m]) for m in range(M_TILES) for a in range(2)]
+            + [(m, 1, a, late[m]) for a in range(2, PASSES) for m in range(M_TILES)]
+        )
+        for m in range(M_TILES):
+            place(m, 1, late[m])
             store(m)

@@ -123,8 +123,8 @@ def tile_list_hscat_none_kernel(tc, x, w_words, w_scales, wgo, offs, out):
             on_scalar(out=result[:], in_=total)
             nc.vector.tensor_tensor(
                 windows[m][:].indirect(offsets[:, LIST_COLS * h : LIST_COLS * (h + 1)]),
-                result[:],
                 weights[:, h * HALF : (h + 1) * HALF],
+                result[:],
                 MULT,
             )
 

from contextlib import ExitStack

import concourse.mybir as mybir

K, M, S, T = 2048, 256, 256, 512
FLOPS = 2 * K * M * S

F32 = mybir.dt.float32
BF16 = mybir.dt.bfloat16
U32 = mybir.dt.uint32
I32 = mybir.dt.int32
U16 = mybir.dt.uint16
U8 = mybir.dt.uint8
FP8X4 = mybir.dt.float8_e4m3fn_x4
MULT = mybir.AluOpType.mult

P = 128
PACK = 4
K_PASS = P * PACK
PASSES = K // K_PASS
LAST = PASSES - 1
HALF = S // 2
PART = HALF // 2
M_TILES = M // P
QUADRANT = 32
SCALE_ROWS = 4
GROUP = 16
LIST_COLS = HALF // GROUP
LINE = 4
ALIGN = 256
WARM_M = 32
EARLY = ((LAST, 0), (0, 0), (0, 1), (1, 0))


def tile_list_hscat_none_kernel(tc, x, w_words, w_scales, wgo, offs, out):
    nc = tc.nc
    with ExitStack() as ctx:
        keep = ctx.enter_context(tc.tile_pool(name="keep", bufs=1))
        psum = ctx.enter_context(tc.psum_pool(name="psum", bufs=1))

        def tile(shape, dtype, name):
            return keep.tile(shape, dtype, name=name, align_bytes=ALIGN)

        windows = [tile([P, T], F32, f"window_{m}") for m in range(M_TILES)]
        for window in windows:
            nc.vector.memset(window[:], 0.0)

        offsets = tile([P, S // GROUP], U16, "offsets")
        x_rows, rounded, x_codes, x_scales, w_codes = {}, {}, {}, {}, {}
        on_vector = nc.vector.tensor_copy
        on_scalar = nc.scalar.copy

        def load_x(a0, a1, h0, h1):
            loaded = tile([P, a1 - a0, PACK, (h1 - h0) * HALF], F32, f"x_rows_{a0}_{h0}")
            rows = x[a0 * K_PASS : a1 * K_PASS, h0 * HALF : h1 * HALF]
            if h1 - h0 == 2:
                nc.sync.dma_start(
                    out=loaded[:].rearrange("p a t j -> p a (t j)"),
                    in_=rows.rearrange("(a p t) j -> p a (t j)", p=P, t=PACK),
                )
            else:
                nc.sync.dma_start(out=loaded[:, 0], in_=rows.rearrange("(p t) j -> p t j", t=PACK))
            for a in range(a0, a1):
                for h in range(h0, h1):
                    x_rows[a, h] = loaded[:, a - a0, :, (h - h0) * HALF : (h - h0 + 1) * HALF]

        def load_w(m, a0, a1):
            loaded = tile([P, a1 - a0, P], U32, f"w_codes_{m}_{a0}")
            words = w_words[a0:a1, :, m * P : (m + 1) * P, :].rearrange("a p n t -> p a (n t)")
            nc.sync.dma_start(out=loaded[:].bitcast(I32), in_=words.bitcast(I32))
            for a in range(a0, a1):
                w_codes[m, a] = loaded[:, a - a0, :]

        def round_cols(a, h, copy, c0=0, c1=HALF):
            if (a, h) not in rounded:
                rounded[a, h] = tile([P, HALF, PACK], BF16, f"rounded_{a}_{h}")
            copy(
                out=rounded[a, h][:, c0:c1, :].rearrange("p (c i) t -> p c t i", i=LINE),
                in_=x_rows[a, h][:, :, c0:c1].rearrange("p t (c i) -> p c t i", i=LINE),
            )

        def round_in_parts(a, h):
            round_cols(a, h, on_vector, 0, PART)
            round_cols(a, h, on_vector, PART, HALF)

        early_codes = tile([P, len(EARLY) * HALF], U32, "early_codes")
        early_scales = tile([P, len(EARLY) * HALF], U8, "early_scales")
        for i, key in enumerate(EARLY):
            x_codes[key] = early_codes[:, i * HALF : (i + 1) * HALF]
            x_scales[key] = early_scales[:, i * HALF : (i + 1) * HALF]

        def quantize(a, h, c0=0, c1=HALF):
            if (a, h) not in x_codes:
                x_codes[a, h] = tile([P, HALF], U32, f"x_codes_{a}_{h}")[:]
                x_scales[a, h] = tile([P, HALF], U8, f"x_scales_{a}_{h}")[:]
            nc.vector.quantize_mx(
                out=x_codes[a, h][:, c0:c1].bitcast(FP8X4),
                scales=x_scales[a, h][:, c0:c1],
                in_=rounded[a, h][:, c0:c1, :].rearrange("p j t -> p (j t)"),
            )

        def quantize_in_parts(a, h):
            quantize(a, h, 0, PART)
            quantize(a, h, PART, HALF)

        def product(m, h, a, total, start=False, stop=False):
            nc.tensor.matmul_mx(
                out=total,
                lhsT=w_codes[m, a].bitcast(FP8X4),
                lhsT_scale=w_scale_rows[SCALE_ROWS * a :, m * P : (m + 1) * P],
                rhs=x_codes[a, h].bitcast(FP8X4),
                rhs_scale=x_scales[a, h],
                start=start,
                stop=stop,
            )

        def group(steps):
            for i, (m, h, a, total) in enumerate(steps):
                product(m, h, a, total, start=i == 0, stop=i == len(steps) - 1)

        def place(m, h, total):
            result = tile([P, HALF], F32, f"y_{m}_{h}")
            on_scalar(out=result[:], in_=total)
            nc.vector.tensor_tensor(
                windows[m][:].indirect(offsets[:, LIST_COLS * h : LIST_COLS * (h + 1)]),
                weights[:, h * HALF : (h + 1) * HALF],
                result[:],
                MULT,
            )

        def store(m):
            nc.sync.dma_start(out=out[m * P : (m + 1) * P, :], in_=windows[m][:])

        w_scale_rows = tile([P, M], U8, "w_scale_rows")
        for quadrant in range(P // QUADRANT):
            rows = slice(QUADRANT * quadrant, QUADRANT * quadrant + PASSES * SCALE_ROWS)
            nc.scalar.dma_start(
                out=w_scale_rows[rows, :].bitcast(I32),
                in_=w_scales[:, SCALE_ROWS * quadrant : SCALE_ROWS * (quadrant + 1), :].bitcast(I32),
            )

        load_x(LAST, PASSES, 0, 1)
        pieces = tile([P, QUADRANT], F32, "weight_pieces")
        nc.sync.dma_start(out=pieces[:], in_=wgo[0:P:8, :].rearrange("s (b c) -> s b c", c=QUADRANT))
        for a in range(LAST):
            load_x(a, a + 1, 0, 2)
        load_w(0, 0, PASSES)
        load_x(LAST, PASSES, 1, 2)
        load_w(1, 2, 4)
        load_w(1, 0, 2)
        nc.sync.dma_start(offsets[:], offs)

        round_cols(LAST, 0, on_scalar)
        quantize(LAST, 0)

        turned = tile([P, QUADRANT], F32, "weights_turned")
        nc.vector.transpose(turned[:], pieces[:])
        repeated = tile([P, S], F32, "weights_repeated")
        nc.vector.tensor_copy(
            out=repeated[:].rearrange("p (b s i) -> p b s i", s=4, i=8),
            in_=turned[:].rearrange("p (s b) -> p b s", b=8).unsqueeze(3).to_broadcast([P, 8, 4, 8]),
        )
        weights = tile([P, S], F32, "weights")
        nc.vector.transpose(weights[:], repeated[:])

        for a in range(LAST):
            round_cols(a, 0, on_vector)
            round_cols(a, 1, on_scalar)
            quantize(a, 0)
            quantize(a, 1)
        round_in_parts(LAST, 1)
        quantize_in_parts(LAST, 1)

        warm_bank = psum.tile([WARM_M, len(EARLY) * HALF], F32, name="warm_bank")
        nc.tensor.matmul_mx(
            out=warm_bank[:],
            lhsT=early_codes[:, :WARM_M].bitcast(FP8X4),
            lhsT_scale=w_scale_rows[:, :WARM_M],
            rhs=early_codes[:].bitcast(FP8X4),
            rhs_scale=early_scales[:],
            start=True,
            stop=True,
        )

        first_sum = psum.tile([P, HALF], F32, name="first_sum")
        group([(0, 0, a, first_sum[:]) for a in (LAST, 0, 1, 2)])
        place(0, 0, first_sum[:])
        second_sum = psum.tile([P, HALF], F32, name="second_sum")
        group([(1, 0, a, second_sum[:]) for a in (2, 3, 0, 1)])
        place(1, 0, second_sum[:])
        late_sums = psum.tile([P, S], F32, name="late_sums")
        late = [late_sums[:, :HALF], late_sums[:, HALF:]]
        group(
            [(m, 1, a, late[m]) for m in range(M_TILES) for a in range(2)]
            + [(m, 1, a, late[m]) for a in range(2, PASSES) for m in range(M_TILES)]
        )
        for m in range(M_TILES):
            place(m, 1, late[m])
            store(m)
